import numpy as np
import ml_dtypes


def mxq(x, axis, fmt="e4m3"):
    dtype, down = {"e4m3": (ml_dtypes.float8_e4m3fn, 7), "e5m2": (ml_dtypes.float8_e5m2, 14)}[fmt]
    v = np.moveaxis(np.asarray(x, np.float32).astype(ml_dtypes.bfloat16).astype(np.float64), axis, -1)
    blocks = v.reshape(v.shape[:-1] + (-1, 32))
    amax = np.abs(blocks).max(-1, keepdims=True)
    byte = np.maximum(np.where(amax > 0, np.frexp(amax)[1] - 1 + 127, 0) - down, 1)
    scale = np.exp2(byte - 127.0)
    codes = (blocks / scale).astype(np.float32).astype(dtype).astype(np.float64)
    return np.moveaxis((codes * scale).reshape(v.shape), -1, axis)


WIDE = False


def mx_kscale(k):
    if not WIDE:
        return np.ones(k)
    levels = np.array([10, -10, 5, -5, 0])
    if k % 512:
        return np.exp2(np.random.permutation(np.resize(levels, k // 32))).repeat(32)
    a = np.empty((k // 512, 16))
    for p in range(k // 512):
        a[p, :8] = np.random.permutation(np.resize(levels, 8))
        for g in range(8):
            far = levels[np.abs(levels - a[p, g]) >= 10]
            a[p, g + 8] = far[np.random.randint(len(far))]
    return np.exp2(a.ravel()).repeat(32)


def f64(x):
    return np.asarray(x).astype(np.float64)


def striped(idx):
    return np.tile(idx.reshape(-1, 16).T, (8, 1)).astype(np.uint16)


def unstriped(offs):
    return offs[:16].T.reshape(-1).astype(np.int64)


E2M1 = np.array([0.0, 0.5, 1.0, 1.5, 2.0, 3.0, 4.0, 6.0, -0.0, -0.5, -1.0, -1.5, -2.0, -3.0, -4.0, -6.0])


def pack_weight(w, fmt):
    k, n = w.shape
    w = f64(np.asarray(w, np.float32).astype(ml_dtypes.bfloat16)).reshape(k // 32, 32, n)
    amax = np.abs(w).max(1)
    if fmt == "e4m3":
        byte = np.frexp(amax)[1] - 1 + 127 - 7
    else:
        mant, ex = np.frexp(amax / 6.0)
        byte = np.where(mant > 0.5, ex, ex - 1) + 127
    byte = np.clip(np.where(amax > 0, byte, 1), 1, 254)
    scaled = (w * np.exp2(127.0 - byte)[:, None, :]).reshape(k, n).astype(np.float32)
    by_word = np.ascontiguousarray(scaled.reshape(k // 512, 128, 4, n).transpose(0, 1, 3, 2))
    if fmt == "e4m3":
        words = by_word.astype(ml_dtypes.float8_e4m3fn).view(np.uint8)
    else:
        c = by_word.astype(ml_dtypes.float4_e2m1fn).view(np.uint8) & 0xF
        words = (c[..., 0::2] | (c[..., 1::2] << 4)).reshape(k // 512, 128, 2 * n)
    return np.ascontiguousarray(words), np.ascontiguousarray(byte.astype(np.uint8).reshape(k // 512, 16, n))


def unpack_weight(words, scales, fmt):
    g, _, n = scales.shape
    words = np.ascontiguousarray(words).reshape(g, 128, n, -1)
    if fmt == "e4m3":
        vals = words.view(ml_dtypes.float8_e4m3fn).astype(np.float64)
    else:
        nib = np.empty((g, 128, n, 4), np.uint8)
        nib[..., 0::2] = words & 0xF
        nib[..., 1::2] = words >> 4
        vals = E2M1[nib]
    vals = vals * np.repeat(np.exp2(scales.astype(np.float64) - 127.0), 8, axis=1)[..., None]
    return vals.transpose(0, 1, 3, 2).reshape(g * 512, n)


def relu2(v):
    return np.maximum(v, 0.0) ** 2


D, T, E, C, H, N = 4, 512, 8, 256, 512, 512


def by_expert(wq, xq):
    return np.concatenate([wq[e].T @ xq[:, e * C:(e + 1) * C] for e in range(E)], axis=1)


def setup_inputs():
    n = np.random.standard_normal
    s = np.tile(mx_kscale(H), D)
    u = mx_kscale(H)
    slot_sub = np.random.permutation(D * T)
    x = pack_weight(n((D * H, T)) * s[:, None], "e4m3")
    w = [pack_weight(m, "e2m1") for m in n((E, H, H)) / np.sqrt(H) / s[None, :H, None] * u]
    wm = pack_weight(n((D * H, N)) / np.sqrt(D * H) / np.tile(u, D)[:, None] ** 2, "e4m3")
    return {
        "x_words": x[0],
        "x_scales": x[1],
        "w_words": np.stack([m[0] for m in w]),
        "w_scales": np.stack([m[1] for m in w]),
        "wm_words": wm[0],
        "wm_scales": wm[1],
        "gate": np.tile(np.random.uniform(0.2, 1.0, E * C), (128, 1)).astype(np.float32),
        "offs": striped(slot_sub),
    }


def reference(x_words, x_scales, w_words, w_scales, wm_words, wm_scales, gate, offs):
    w = np.stack([unpack_weight(w_words[e], w_scales[e], "e2m1") for e in range(E)])
    wm = unpack_weight(wm_words, wm_scales, "e4m3")
    idx = unstriped(offs)
    x = unpack_weight(x_words, x_scales, "e4m3")
    sub = x.reshape(D, H, T).transpose(1, 0, 2).reshape(H, D * T)
    y = relu2(by_expert(w, sub[:, idx]))
    c = np.zeros((H, D * T))
    c[:, idx] = f64(gate[:1]) * y
    cq = mxq(c, 0, "e4m3").reshape(H, D, T).transpose(1, 0, 2).reshape(D * H, T)
    return wm.T @ cq

@@ -1,0 +1,176 @@
+from contextlib import ExitStack
+
+import concourse.mybir as mybir
+from concourse.masks import make_identity
+
+HEADS, TOKENS, EXPERTS, CAP, WIDTH, N_OUT = 4, 512, 8, 256, 512, 512
+SLOTS = EXPERTS * CAP
+P = 128
+PACK = 4
+FLOPS = 2 * WIDTH * WIDTH * SLOTS + 2 * HEADS * WIDTH * N_OUT * TOKENS
+BYTES = 4 * 1048576 + 524288 + 2 * 32768 + 65536 + 32768
+
+F32 = mybir.dt.float32
+BF16 = mybir.dt.bfloat16
+I32 = mybir.dt.int32
+U32 = mybir.dt.uint32
+U16 = mybir.dt.uint16
+U8 = mybir.dt.uint8
+FP8X4 = mybir.dt.float8_e4m3fn_x4
+FP4X4 = mybir.dt.float4_e2m1fn_x4
+ACT = mybir.ActivationFunctionType
+MULT = mybir.AluOpType.mult
+
+GATHERS = (("words", 0, 1024), ("bytes", 0, 512), ("words", 1024, 2048), ("bytes", 512, 1024), ("bytes", 1024, 2048))
+SCATTERS = ((2, 0), (0, 0), (2, 1), (1, 0), (2, 2), (0, 1), (2, 3), (0, 2), (1, 1), (0, 3), (1, 2), (3, 0), (1, 3), (3, 1), (3, 2), (3, 3))
+CHUNK = 128
+CHUNKS = TOKENS // CHUNK
+PIECE = 512
+STAGES = 4
+AHEAD = 2
+VECTOR_CHUNKS = (0, 1)
+
+
+def tile_moe_mhm_relu2_kernel(
+    tc, x_words, x_scales, w_words, w_scales, wm_words, wm_scales, gate, offs, out
+):
+    nc = tc.nc
+    with ExitStack() as ctx:
+        keep = ctx.enter_context(tc.tile_pool(name="keep", bufs=1))
+        ring = ctx.enter_context(tc.tile_pool(name="ring", bufs=3))
+        ps_y = ctx.enter_context(tc.psum_pool(name="ps_y", bufs=2))
+        ps_t = ctx.enter_context(tc.psum_pool(name="ps_t", bufs=1))
+        ps_o = ctx.enter_context(tc.psum_pool(name="ps_o", bufs=4))
+
+        offsets = keep.tile([P, SLOTS // 16], U16, name="offsets")
+        xw = keep.tile([P, SLOTS], I32, name="xw", align_bytes=64)
+        xs = keep.tile([P, SLOTS], U8, name="xs", align_bytes=64)
+        ww = keep.tile([P, EXPERTS, 2 * WIDTH], U8, name="ww", align_bytes=64)
+        ws = keep.tile([P, EXPERTS * WIDTH], U8, name="ws", align_bytes=64)
+        ident = keep.tile([P, P], F32, name="ident")
+        gw = keep.tile([P, SLOTS], U32, name="gw", align_bytes=64)
+        gs = keep.tile([P, SLOTS], U8, name="gs", align_bytes=64)
+        y = keep.tile([P, STAGES, PIECE], F32, name="y")
+        r = keep.tile([P, SLOTS // P, PACK, P], F32, name="r")
+        banks = [ps_t.tile([P, PIECE], F32, name=f"bank{b}") for b in range(2)]
+        windows = [keep.tile([P, SLOTS], F32, name=f"window{d}") for d in range(PACK)]
+        grouped = keep.tile([P, CHUNKS, HEADS, CHUNK, PACK], BF16, name="grouped", align_bytes=64)
+
+        nc.gpsimd.memset(xs[:].bitcast(I32), 0)
+        nc.vector.memset(ws[:].bitcast(I32), 0)
+        make_identity(nc, ident[:])
+
+        nc.sync.dma_start(offsets[:], offs)
+        nc.sync.dma_start(
+            xw[:].rearrange("p (o t) -> p o t", o=HEADS),
+            x_words.rearrange("o p t d -> p o (t d)").bitcast(I32),
+        )
+        nc.sync.dma_start(ww[:].bitcast(I32), w_words.rearrange("e s p b -> p (e s) b").bitcast(I32))
+        xs_rows = x_scales.bitcast(I32)
+        xs_view = xs[:].bitcast(I32).rearrange("p (o t) -> p o t", o=HEADS)
+        for q in range(4):
+            nc.sync.dma_start(xs_view[32 * q : 32 * q + 4], xs_rows[:, 4 * q : 4 * q + 4, :].rearrange("o r t -> r o t"))
+        ws_rows = w_scales.rearrange("e s b l -> (e s) b l").bitcast(I32)
+        ws_view = ws[:].bitcast(I32).rearrange("p (e l) -> p e l", e=EXPERTS)
+        for q in range(4):
+            nc.sync.dma_start(ws_view[32 * q : 32 * q + 4], ws_rows[:, 4 * q : 4 * q + 4, :].rearrange("e r l -> r e l"))
+
+        def listed(j0, j1):
+            return offsets[:, j0 // 16 : j1 // 16]
+
+        for sort, j0, j1 in GATHERS:
+            if sort == "bytes":
+                nc.vector.tensor_copy(gs[:, j0:j1], xs[:].indirect(listed(j0, j1)))
+            else:
+                nc.vector.tensor_copy(gw[:, j0:j1], xw[:].bitcast(U32).indirect(listed(j0, j1)))
+
+        gates = keep.tile([P, SLOTS], F32, name="xw", align_bytes=64)
+        for j0, j1 in ((0, PIECE), (PIECE, SLOTS)):
+            nc.sync.dma_start(gates[:, j0:j1], gate[:, j0:j1])
+
+        def product(s):
+            e = s * P // CAP
+            slots = slice(s * P, (s + 1) * P)
+            v = ps_y.tile([P, WIDTH], F32, name="v")
+            nc.tensor.matmul_mx(
+                out=v[:],
+                lhsT=gw[:, slots].bitcast(FP8X4),
+                lhsT_scale=gs[:, slots],
+                rhs=ww[:, e, :].bitcast(FP4X4),
+                rhs_scale=ws[:, e * WIDTH : (e + 1) * WIDTH],
+                start=True,
+                stop=True,
+            )
+            nc.scalar.activation(r[:, s], v[:].rearrange("j (p d) -> j d p", d=PACK), ACT.Relu)
+
+        def turn(k):
+            d, part = SCATTERS[k]
+            bank = banks[k % len(banks)]
+            for i in range(PIECE // P):
+                nc.tensor.transpose(bank[:, i * P : (i + 1) * P], r[:, part * (PIECE // P) + i, d, :], ident[:])
+            nc.scalar.activation(y[:, k % STAGES, :], bank[:], ACT.Square)
+
+        def plane(d, h0, h1):
+            src = windows[d][:].rearrange("p (o h t) -> p h o t", o=HEADS, h=CHUNKS)
+            return grouped[:, h0:h1, :, :, d], src[:, h0:h1]
+
+        multiplied = 0
+        waiting = []
+        for k in range(-AHEAD, len(SCATTERS)):
+            if k + AHEAD < len(SCATTERS):
+                while multiplied <= SCATTERS[k + AHEAD][1]:
+                    for i in range(PIECE // P):
+                        product(multiplied * (PIECE // P) + i)
+                    multiplied += 1
+                turn(k + AHEAD)
+            if k < 0:
+                continue
+            d, part = SCATTERS[k]
+            j0, j1 = part * PIECE, (part + 1) * PIECE
+            nc.vector.tensor_tensor(windows[d][:].indirect(listed(j0, j1)), y[:, k % STAGES, :], gates[:, j0:j1], MULT)
+            if part == SLOTS // PIECE - 1 and d < PACK - 1:
+                waiting.extend([(d, 0, CHUNKS // 2), (d, CHUNKS // 2, CHUNKS)])
+            if waiting:
+                nc.scalar.copy(*plane(*waiting.pop(0)))
+
+        mw = keep.tile([P, HEADS, N_OUT], I32, name="ww", align_bytes=64)
+        ms = keep.tile([P, N_OUT], U8, name="ws", align_bytes=64)
+        nc.gpsimd.memset(ms[:].bitcast(I32), 0)
+        ms_rows = wm_scales.bitcast(I32)
+        for q in range(4):
+            nc.sync.dma_start(ms[32 * q : 32 * q + 16, :].bitcast(I32), ms_rows[:, 4 * q : 4 * q + 4, :])
+        nc.sync.dma_start(mw[:], wm_words.rearrange("s p n d -> p s (n d)").bitcast(I32))
+
+        for h in range(CHUNKS):
+            if h in VECTOR_CHUNKS:
+                nc.vector.tensor_copy(*plane(PACK - 1, h, h + 1))
+            else:
+                nc.scalar.copy(*plane(PACK - 1, h, h + 1))
+
+        out_view = out.rearrange("(m p) t -> p m t", p=P)
+        per_bank = 512 // CHUNK
+        for h in range(CHUNKS):
+            cw = keep.tile([P, HEADS, CHUNK], U32, name=f"cw{h}", align_bytes=64)
+            cs = keep.tile([P, HEADS, CHUNK], U8, name=f"cs{h}", align_bytes=64)
+            nc.vector.quantize_mx(
+                out=cw[:].rearrange("p o t -> p (o t)").bitcast(FP8X4),
+                scales=cs[:].rearrange("p o t -> p (o t)"),
+                in_=grouped[:, h].rearrange("p o t d -> p (o t d)"),
+            )
+            for m0 in range(0, N_OUT // P, per_bank):
+                acc = ps_o.tile([P, per_bank, CHUNK], F32, name="acc")
+                for i in range(per_bank):
+                    cols = slice((m0 + i) * P, (m0 + i + 1) * P)
+                    for o in range(HEADS):
+                        nc.tensor.matmul_mx(
+                            out=acc[:, i, :],
+                            lhsT=mw[:, o, cols].bitcast(FP8X4),
+                            lhsT_scale=ms[4 * o :, cols],
+                            rhs=cw[:, o, :].bitcast(FP8X4),
+                            rhs_scale=cs[:, o, :],
+                            start=(o == 0),
+                            stop=(o == HEADS - 1),
+                        )
+                res = ring.tile([P, per_bank, CHUNK], F32, name="res")
+                nc.scalar.copy(res[:], acc[:])
+                nc.sync.dma_start(out_view[:, m0 : m0 + per_bank, h * CHUNK : (h + 1) * CHUNK], res[:])

@@ -21,14 +21,16 @@ FP4X4 = mybir.dt.float4_e2m1fn_x4
 ACT = mybir.ActivationFunctionType
 MULT = mybir.AluOpType.mult
 
-GATHERS = (("words", 0, 1024), ("bytes", 0, 512), ("words", 1024, 2048), ("bytes", 512, 1024), ("bytes", 1024, 2048))
-SCATTERS = ((2, 0), (0, 0), (2, 1), (1, 0), (2, 2), (0, 1), (2, 3), (0, 2), (1, 1), (0, 3), (1, 2), (3, 0), (1, 3), (3, 1), (3, 2), (3, 3))
+GATHERS = (("bytes", 0, 1024), ("bytes", 1024, 2048), ("words", 0, 256), ("words", 256, 1024), ("words", 1024, 2048))
+SCATTERS = ((2, 0, 256), (0, 0, 256), (1, 0, 256), (2, 256, 1024), (0, 256, 1024), (2, 1024, 2048), (0, 1024, 2048), (1, 256, 1280), (3, 0, 512), (1, 1280, 2048), (3, 512, 1536), (3, 1536, 1792), (3, 1792, 2048))
+BANK = 512
+STAGES = 3
+AHEAD = 2
 CHUNK = 128
 CHUNKS = TOKENS // CHUNK
-PIECE = 512
-STAGES = 4
-AHEAD = 2
-VECTOR_CHUNKS = (0, 1)
+VECTOR_HEADS = (3, 2, 0, 0)
+VECTOR_OUT = ((0, 0), (1, 0), (3, 2))
+WARM = 8
 
 
 def tile_moe_mhm_relu2_kernel(
@@ -37,10 +39,9 @@ def tile_moe_mhm_relu2_kernel(
     nc = tc.nc
     with ExitStack() as ctx:
         keep = ctx.enter_context(tc.tile_pool(name="keep", bufs=1))
-        ring = ctx.enter_context(tc.tile_pool(name="ring", bufs=3))
-        ps_y = ctx.enter_context(tc.psum_pool(name="ps_y", bufs=2))
+        ring = ctx.enter_context(tc.tile_pool(name="ring", bufs=6))
+        ps_y = ctx.enter_context(tc.psum_pool(name="ps_y", bufs=5))
         ps_t = ctx.enter_context(tc.psum_pool(name="ps_t", bufs=1))
-        ps_o = ctx.enter_context(tc.psum_pool(name="ps_o", bufs=4))
 
         offsets = keep.tile([P, SLOTS // 16], U16, name="offsets")
         xw = keep.tile([P, SLOTS], I32, name="xw", align_bytes=64)
@@ -50,22 +51,21 @@ def tile_moe_mhm_relu2_kernel(
         ident = keep.tile([P, P], F32, name="ident")
         gw = keep.tile([P, SLOTS], U32, name="gw", align_bytes=64)
         gs = keep.tile([P, SLOTS], U8, name="gs", align_bytes=64)
-        y = keep.tile([P, STAGES, PIECE], F32, name="y")
+        y = keep.tile([P, STAGES, 2 * BANK], F32, name="y")
         r = keep.tile([P, SLOTS // P, PACK, P], F32, name="r")
-        banks = [ps_t.tile([P, PIECE], F32, name=f"bank{b}") for b in range(2)]
+        banks = [ps_t.tile([P, BANK], F32, name=f"bank{b}") for b in range(3)]
         windows = [keep.tile([P, SLOTS], F32, name=f"window{d}") for d in range(PACK)]
         grouped = keep.tile([P, CHUNKS, HEADS, CHUNK, PACK], BF16, name="grouped", align_bytes=64)
 
         nc.gpsimd.memset(xs[:].bitcast(I32), 0)
         nc.vector.memset(ws[:].bitcast(I32), 0)
-        make_identity(nc, ident[:])
-
         nc.sync.dma_start(offsets[:], offs)
-        nc.sync.dma_start(
+        nc.gpsimd.dma_start(
             xw[:].rearrange("p (o t) -> p o t", o=HEADS),
             x_words.rearrange("o p t d -> p o (t d)").bitcast(I32),
         )
-        nc.sync.dma_start(ww[:].bitcast(I32), w_words.rearrange("e s p b -> p (e s) b").bitcast(I32))
+        nc.gpsimd.dma_start(ww[:].bitcast(I32), w_words.rearrange("e s p b -> p (e s) b").bitcast(I32))
+        make_identity(nc, ident[:])
         xs_rows = x_scales.bitcast(I32)
         xs_view = xs[:].bitcast(I32).rearrange("p (o t) -> p o t", o=HEADS)
         for q in range(4):
@@ -84,8 +84,8 @@ def tile_moe_mhm_relu2_kernel(
             else:
                 nc.vector.tensor_copy(gw[:, j0:j1], xw[:].bitcast(U32).indirect(listed(j0, j1)))
 
-        gates = keep.tile([P, SLOTS], F32, name="xw", align_bytes=64)
-        for j0, j1 in ((0, PIECE), (PIECE, SLOTS)):
+        gates = keep.tile([P, SLOTS], F32, name="xs", align_bytes=64)
+        for j0, j1 in ((0, BANK), (BANK, SLOTS)):
             nc.sync.dma_start(gates[:, j0:j1], gate[:, j0:j1])
 
         def product(s):
@@ -103,34 +103,38 @@ def tile_moe_mhm_relu2_kernel(
             )
             nc.scalar.activation(r[:, s], v[:].rearrange("j (p d) -> j d p", d=PACK), ACT.Relu)
 
-        def turn(k):
-            d, part = SCATTERS[k]
-            bank = banks[k % len(banks)]
-            for i in range(PIECE // P):
-                nc.tensor.transpose(bank[:, i * P : (i + 1) * P], r[:, part * (PIECE // P) + i, d, :], ident[:])
-            nc.scalar.activation(y[:, k % STAGES, :], bank[:], ACT.Square)
+        def stage(k):
+            d, j0, j1 = SCATTERS[k]
+            return y[:, (k - 2 if k == len(SCATTERS) - 1 else k) % STAGES, 0 : j1 - j0]
 
-        def plane(d, h0, h1):
+        def turn(k):
+            d, j0, j1 = SCATTERS[k]
+            for a in range(j0, j1, BANK):
+                b = min(a + BANK, j1)
+                banks.append(banks.pop(0))
+                for j in range(a, b, P):
+                    nc.tensor.transpose(banks[0][:, j - a : j - a + P], r[:, j // P, d, :], ident[:])
+                nc.scalar.activation(stage(k)[:, a - j0 : b - j0], banks[0][:, 0 : b - a], ACT.Square)
+
+
+        def plane(d, h0, h1, o0=0, o1=HEADS):
             src = windows[d][:].rearrange("p (o h t) -> p h o t", o=HEADS, h=CHUNKS)
-            return grouped[:, h0:h1, :, :, d], src[:, h0:h1]
+            return grouped[:, h0:h1, o0:o1, :, d], src[:, h0:h1, o0:o1]
 
         multiplied = 0
+        turned = 0
         waiting = []
-        for k in range(-AHEAD, len(SCATTERS)):
-            if k + AHEAD < len(SCATTERS):
-                while multiplied <= SCATTERS[k + AHEAD][1]:
-                    for i in range(PIECE // P):
-                        product(multiplied * (PIECE // P) + i)
+        for k, (d, j0, j1) in enumerate(SCATTERS):
+            while turned < len(SCATTERS) and turned <= k + (1 if k >= len(SCATTERS) - 3 else AHEAD):
+                while multiplied * P < SCATTERS[turned][2]:
+                    product(multiplied)
                     multiplied += 1
-                turn(k + AHEAD)
-            if k < 0:
-                continue
-            d, part = SCATTERS[k]
-            j0, j1 = part * PIECE, (part + 1) * PIECE
-            nc.vector.tensor_tensor(windows[d][:].indirect(listed(j0, j1)), y[:, k % STAGES, :], gates[:, j0:j1], MULT)
-            if part == SLOTS // PIECE - 1 and d < PACK - 1:
-                waiting.extend([(d, 0, CHUNKS // 2), (d, CHUNKS // 2, CHUNKS)])
-            if waiting:
+                turn(turned)
+                turned += 1
+            nc.vector.tensor_tensor(windows[d][:].indirect(listed(j0, j1)), stage(k), gates[:, j0:j1], MULT)
+            if j1 == SLOTS and d < PACK - 1:
+                waiting.extend((d, h, h + 1) for h in range(CHUNKS))
+            while len(waiting) > (1 if len(SCATTERS) - 4 <= k < len(SCATTERS) - 2 else 0):
                 nc.scalar.copy(*plane(*waiting.pop(0)))
 
         mw = keep.tile([P, HEADS, N_OUT], I32, name="ww", align_bytes=64)
@@ -141,14 +145,25 @@ def tile_moe_mhm_relu2_kernel(
             nc.sync.dma_start(ms[32 * q : 32 * q + 16, :].bitcast(I32), ms_rows[:, 4 * q : 4 * q + 4, :])
         nc.sync.dma_start(mw[:], wm_words.rearrange("s p n d -> p s (n d)").bitcast(I32))
 
-        for h in range(CHUNKS):
-            if h in VECTOR_CHUNKS:
-                nc.vector.tensor_copy(*plane(PACK - 1, h, h + 1))
-            else:
-                nc.scalar.copy(*plane(PACK - 1, h, h + 1))
+        for i in range(WARM):
+            nc.tensor.matmul_mx(
+                out=banks[0][:],
+                lhsT=mw[:, 0, 0:P].bitcast(FP8X4),
+                lhsT_scale=ms[:, 0:P],
+                rhs=mw[:, 0, :].bitcast(FP8X4),
+                rhs_scale=ms[:],
+                start=True,
+                stop=True,
+            )
 
-        out_view = out.rearrange("(m p) t -> p m t", p=P)
-        per_bank = 512 // CHUNK
+        for h in range(CHUNKS):
+            split = VECTOR_HEADS[h]
+            if split > 0:
+                nc.vector.tensor_copy(*plane(PACK - 1, h, h + 1, 0, split))
+            if split < HEADS:
+                nc.scalar.copy(*plane(PACK - 1, h, h + 1, split, HEADS))
+
+        codes = []
         for h in range(CHUNKS):
             cw = keep.tile([P, HEADS, CHUNK], U32, name=f"cw{h}", align_bytes=64)
             cs = keep.tile([P, HEADS, CHUNK], U8, name=f"cs{h}", align_bytes=64)
@@ -157,13 +172,19 @@ def tile_moe_mhm_relu2_kernel(
                 scales=cs[:].rearrange("p o t -> p (o t)"),
                 in_=grouped[:, h].rearrange("p o t d -> p (o t d)"),
             )
-            for m0 in range(0, N_OUT // P, per_bank):
-                acc = ps_o.tile([P, per_bank, CHUNK], F32, name="acc")
-                for i in range(per_bank):
-                    cols = slice((m0 + i) * P, (m0 + i + 1) * P)
+            codes.append((cw, cs))
+
+        out_view = out.rearrange("(m p) t -> p m t", p=P)
+        for h, (cw, cs) in enumerate(codes):
+            tokens = slice(h * CHUNK, (h + 1) * CHUNK)
+            parts = ((0, 2), (2, 4)) if h == CHUNKS - 1 else ((0, 4),)
+            for m0, m1 in parts:
+                acc = ps_y.tile([P, m1 - m0, CHUNK], F32, name="v")
+                for m in range(m0, m1):
+                    cols = slice(m * P, (m + 1) * P)
                     for o in range(HEADS):
                         nc.tensor.matmul_mx(
-                            out=acc[:, i, :],
+                            out=acc[:, m - m0, :],
                             lhsT=mw[:, o, cols].bitcast(FP8X4),
                             lhsT_scale=ms[4 * o :, cols],
                             rhs=cw[:, o, :].bitcast(FP8X4),
@@ -171,6 +192,9 @@ def tile_moe_mhm_relu2_kernel(
                             start=(o == 0),
                             stop=(o == HEADS - 1),
                         )
-                res = ring.tile([P, per_bank, CHUNK], F32, name="res")
-                nc.scalar.copy(res[:], acc[:])
-                nc.sync.dma_start(out_view[:, m0 : m0 + per_bank, h * CHUNK : (h + 1) * CHUNK], res[:])
+                res = ring.tile([P, m1 - m0, CHUNK], F32, name="res")
+                if (h, m0) in VECTOR_OUT:
+                    nc.vector.tensor_copy(res[:], acc[:])
+                else:
+                    nc.scalar.copy(res[:], acc[:])
+                nc.sync.dma_start(out_view[:, m0:m1, tokens], res[:])

@@ -20,17 +20,20 @@ FP8X4 = mybir.dt.float8_e4m3fn_x4
 FP4X4 = mybir.dt.float4_e2m1fn_x4
 ACT = mybir.ActivationFunctionType
 MULT = mybir.AluOpType.mult
+ADD = mybir.AluOpType.add
 
 GATHERS = (("bytes", 0, 1024), ("bytes", 1024, 2048), ("words", 0, 256), ("words", 256, 1024), ("words", 1024, 2048))
-SCATTERS = ((2, 0, 256), (0, 0, 256), (1, 0, 256), (2, 256, 1024), (0, 256, 1024), (2, 1024, 2048), (0, 1024, 2048), (1, 256, 1280), (3, 0, 512), (1, 1280, 2048), (3, 512, 1536), (3, 1536, 1792), (3, 1792, 2048))
+SCATTERS = ((0, 0, 256), (0, 256, 512), (1, 0, 512), (0, 512, 1024), (1, 512, 1024), (0, 1024, 1536), (0, 1536, 2048), (1, 1024, 1536), (1, 1536, 2048))
 BANK = 512
-STAGES = 3
-AHEAD = 2
+PAIRS = 2
+HALF = WIDTH // PAIRS
+TILES = SLOTS // P
 CHUNK = 128
 CHUNKS = TOKENS // CHUNK
 VECTOR_HEADS = (3, 2, 0, 0)
 VECTOR_OUT = ((0, 0), (1, 0), (3, 2))
-WARM = 8
+SCALAR_CHUNKS = 2
+LENDERS = (14, 15, 12, 13)
 
 
 def tile_moe_mhm_relu2_kernel(
@@ -51,11 +54,11 @@ def tile_moe_mhm_relu2_kernel(
         ident = keep.tile([P, P], F32, name="ident")
         gw = keep.tile([P, SLOTS], U32, name="gw", align_bytes=64)
         gs = keep.tile([P, SLOTS], U8, name="gs", align_bytes=64)
-        y = keep.tile([P, STAGES, 2 * BANK], F32, name="y")
-        r = keep.tile([P, SLOTS // P, PACK, P], F32, name="r")
+        r = keep.tile([P, TILES, PAIRS, HALF], F32, name="r")
+        gate_rows = keep.tile([P, P], F32, name="gate_rows")
+        gate_cols = keep.tile([P, TILES], F32, name="gate_cols")
         banks = [ps_t.tile([P, BANK], F32, name=f"bank{b}") for b in range(3)]
-        windows = [keep.tile([P, SLOTS], F32, name=f"window{d}") for d in range(PACK)]
-        grouped = keep.tile([P, CHUNKS, HEADS, CHUNK, PACK], BF16, name="grouped", align_bytes=64)
+        windows = [keep.tile([P, SLOTS], F32, name=f"window{d}") for d in range(PAIRS)]
 
         nc.gpsimd.memset(xs[:].bitcast(I32), 0)
         nc.vector.memset(ws[:].bitcast(I32), 0)
@@ -66,6 +69,7 @@ def tile_moe_mhm_relu2_kernel(
         )
         nc.gpsimd.dma_start(ww[:].bitcast(I32), w_words.rearrange("e s p b -> p (e s) b").bitcast(I32))
         make_identity(nc, ident[:])
+        nc.gpsimd.memset(gate_rows[:], 0.0)
         xs_rows = x_scales.bitcast(I32)
         xs_view = xs[:].bitcast(I32).rearrange("p (o t) -> p o t", o=HEADS)
         for q in range(4):
@@ -84,9 +88,9 @@ def tile_moe_mhm_relu2_kernel(
             else:
                 nc.vector.tensor_copy(gw[:, j0:j1], xw[:].bitcast(U32).indirect(listed(j0, j1)))
 
-        gates = keep.tile([P, SLOTS], F32, name="xs", align_bytes=64)
-        for j0, j1 in ((0, BANK), (BANK, SLOTS)):
-            nc.sync.dma_start(gates[:, j0:j1], gate[:, j0:j1])
+        nc.sync.dma_start(gate_rows[0:TILES, :], gate[0:1, :].rearrange("r (s j) -> (r s) j", j=P))
+        nc.tensor.transpose(banks[2][:, 0:P], gate_rows[:], ident[:])
+        nc.scalar.copy(gate_cols[:], banks[2][:, 0:TILES])
 
         def product(s):
             e = s * P // CAP
@@ -101,41 +105,43 @@ def tile_moe_mhm_relu2_kernel(
                 start=True,
                 stop=True,
             )
-            nc.scalar.activation(r[:, s], v[:].rearrange("j (p d) -> j d p", d=PACK), ACT.Relu)
-
-        def stage(k):
-            d, j0, j1 = SCATTERS[k]
-            return y[:, (k - 2 if k == len(SCATTERS) - 1 else k) % STAGES, 0 : j1 - j0]
-
-        def turn(k):
-            d, j0, j1 = SCATTERS[k]
-            for a in range(j0, j1, BANK):
-                b = min(a + BANK, j1)
-                banks.append(banks.pop(0))
-                for j in range(a, b, P):
-                    nc.tensor.transpose(banks[0][:, j - a : j - a + P], r[:, j // P, d, :], ident[:])
-                nc.scalar.activation(stage(k)[:, a - j0 : b - j0], banks[0][:, 0 : b - a], ACT.Square)
-
-
-        def plane(d, h0, h1, o0=0, o1=HEADS):
-            src = windows[d][:].rearrange("p (o h t) -> p h o t", o=HEADS, h=CHUNKS)
-            return grouped[:, h0:h1, o0:o1, :, d], src[:, h0:h1, o0:o1]
+            nc.scalar.activation(
+                r[:, s].rearrange("j u (p e) -> j u p e", e=PAIRS),
+                v[:].rearrange("j (p u e) -> j u p e", u=PAIRS, e=PAIRS),
+                ACT.Relu,
+            )
 
         multiplied = 0
-        turned = 0
-        waiting = []
-        for k, (d, j0, j1) in enumerate(SCATTERS):
-            while turned < len(SCATTERS) and turned <= k + (1 if k >= len(SCATTERS) - 3 else AHEAD):
-                while multiplied * P < SCATTERS[turned][2]:
-                    product(multiplied)
-                    multiplied += 1
-                turn(turned)
-                turned += 1
-            nc.vector.tensor_tensor(windows[d][:].indirect(listed(j0, j1)), stage(k), gates[:, j0:j1], MULT)
-            if j1 == SLOTS and d < PACK - 1:
-                waiting.extend((d, h, h + 1) for h in range(CHUNKS))
-            while len(waiting) > (1 if len(SCATTERS) - 4 <= k < len(SCATTERS) - 2 else 0):
-                nc.scalar.copy(*plane(*waiting.pop(0)))
+        for k, (u, j0, j1) in enumerate(SCATTERS):
+            s0, s1 = j0 // P, j1 // P
+            while multiplied < s1:
+                product(multiplied)
+                multiplied += 1
+            y = keep.tile([P, s1 - s0, HALF], F32, name=f"y{k}")
+            nc.scalar.activation(y[:], r[:, s0:s1, u, :], ACT.Square)
+            banks.append(banks.pop(0))
+            for s in range(s0, s1):
+                pairs = keep.tile([P, HALF], BF16, name=f"pairs{s}_{u}", align_bytes=64)
+                nc.gpsimd.tensor_scalar(pairs[:], y[:, s - s0, :], gate_cols[:, s : s + 1], 0.0, MULT, ADD)
+                nc.tensor.transpose(banks[0][:, (s - s0) * P : (s - s0 + 1) * P], pairs[:].bitcast(F32), ident[:])
+            stage = keep.tile([P, j1 - j0], F32, name=f"stage{k}")
+            nc.scalar.copy(stage[:], banks[0][:, 0 : j1 - j0])
+            nc.vector.tensor_copy(windows[u][:].indirect(listed(j0, j1)), stage[:])
+
+        grouped = [
+            keep.tile([P, HEADS, CHUNK, PAIRS], U32, name=f"pairs{LENDERS[h]}_1", align_bytes=64) for h in range(CHUNKS)
+        ]
+
+        def plane(u, h, o0, o1, dtype):
+            src = windows[u][:].bitcast(dtype).rearrange("p (o h t) -> p h o t", o=HEADS, h=CHUNKS)
+            dst = grouped[h][:].rearrange("p o t u -> p (o t u)").bitcast(dtype).rearrange("p (o t u) -> p o t u", o=HEADS, u=PAIRS)
+            return dst[:, o0:o1, :, u], src[:, h, o0:o1]
+
+        for h in range(CHUNKS):
+            if h < SCALAR_CHUNKS:
+                nc.scalar.copy(*plane(0, h, 0, HEADS, U32))
+            else:
+                nc.gpsimd.tensor_copy(*plane(0, h, 0, HEADS, U32))
 
         mw = keep.tile([P, HEADS, N_OUT], I32, name="ww", align_bytes=64)
         ms = keep.tile([P, N_OUT], U8, name="ws", align_bytes=64)
@@ -145,23 +151,12 @@ def tile_moe_mhm_relu2_kernel(
             nc.sync.dma_start(ms[32 * q : 32 * q + 16, :].bitcast(I32), ms_rows[:, 4 * q : 4 * q + 4, :])
         nc.sync.dma_start(mw[:], wm_words.rearrange("s p n d -> p s (n d)").bitcast(I32))
 
-        for i in range(WARM):
-            nc.tensor.matmul_mx(
-                out=banks[0][:],
-                lhsT=mw[:, 0, 0:P].bitcast(FP8X4),
-                lhsT_scale=ms[:, 0:P],
-                rhs=mw[:, 0, :].bitcast(FP8X4),
-                rhs_scale=ms[:],
-                start=True,
-                stop=True,
-            )
-
         for h in range(CHUNKS):
             split = VECTOR_HEADS[h]
             if split > 0:
-                nc.vector.tensor_copy(*plane(PACK - 1, h, h + 1, 0, split))
+                nc.vector.tensor_copy(*plane(1, h, 0, split, I32))
             if split < HEADS:
-                nc.scalar.copy(*plane(PACK - 1, h, h + 1, split, HEADS))
+                nc.scalar.copy(*plane(1, h, split, HEADS, U32))
 
         codes = []
         for h in range(CHUNKS):
@@ -170,7 +165,7 @@ def tile_moe_mhm_relu2_kernel(
             nc.vector.quantize_mx(
                 out=cw[:].rearrange("p o t -> p (o t)").bitcast(FP8X4),
                 scales=cs[:].rearrange("p o t -> p (o t)"),
-                in_=grouped[:, h].rearrange("p o t d -> p (o t d)"),
+                in_=grouped[h][:].rearrange("p o t u -> p (o t u)").bitcast(BF16),
             )
             codes.append((cw, cs))
 

@@ -22,8 +22,11 @@ ACT = mybir.ActivationFunctionType
 MULT = mybir.AluOpType.mult
 ADD = mybir.AluOpType.add
 
-GATHERS = (("bytes", 0, 1024), ("bytes", 1024, 2048), ("words", 0, 256), ("words", 256, 1024), ("words", 1024, 2048))
-SCATTERS = ((0, 0, 256), (0, 256, 512), (1, 0, 512), (0, 512, 1024), (1, 512, 1024), (0, 1024, 1536), (0, 1536, 2048), (1, 1024, 1536), (1, 1536, 2048))
+EARLY_BYTES = 1536
+PIECES = ((0, 0, 256), (1, 0, 256), (0, 256, 512), (1, 256, 512), (0, 512, 1024), (1, 512, 768), (0, 1024, 1536), (1, 768, 1024), (0, 1536, 2048), (1, 1024, 1536), (1, 1536, 2048))
+AHEAD = 0
+FINE = 1
+FIRST_EXPERTS = 2
 BANK = 512
 PAIRS = 2
 HALF = WIDTH // PAIRS
@@ -32,8 +35,9 @@ CHUNK = 128
 CHUNKS = TOKENS // CHUNK
 VECTOR_HEADS = (3, 2, 0, 0)
 VECTOR_OUT = ((0, 0), (1, 0), (3, 2))
-SCALAR_CHUNKS = 2
-LENDERS = (14, 15, 12, 13)
+WARM = 0
+HELD = 0
+CHUNK_WORDS = HEADS * CHUNK * PAIRS
 
 
 def tile_moe_mhm_relu2_kernel(
@@ -49,14 +53,15 @@ def tile_moe_mhm_relu2_kernel(
         offsets = keep.tile([P, SLOTS // 16], U16, name="offsets")
         xw = keep.tile([P, SLOTS], I32, name="xw", align_bytes=64)
         xs = keep.tile([P, SLOTS], U8, name="xs", align_bytes=64)
-        ww = keep.tile([P, EXPERTS, 2 * WIDTH], U8, name="ww", align_bytes=64)
+        ww_first = keep.tile([P, FIRST_EXPERTS, 2 * WIDTH], U8, name="ww_first", align_bytes=64)
+        ww_rest = keep.tile([P, EXPERTS - FIRST_EXPERTS, 2 * WIDTH], U8, name="ww", align_bytes=64)
         ws = keep.tile([P, EXPERTS * WIDTH], U8, name="ws", align_bytes=64)
         ident = keep.tile([P, P], F32, name="ident")
-        gw = keep.tile([P, SLOTS], U32, name="gw", align_bytes=64)
-        gs = keep.tile([P, SLOTS], U8, name="gs", align_bytes=64)
-        r = keep.tile([P, TILES, PAIRS, HALF], F32, name="r")
-        gate_rows = keep.tile([P, P], F32, name="gate_rows")
-        gate_cols = keep.tile([P, TILES], F32, name="gate_cols")
+        gw_first = keep.tile([P, CAP], U32, name="gw_first", align_bytes=64)
+        gw = keep.tile([P, SLOTS - CAP], U32, name="gw", align_bytes=64)
+        gs = keep.tile([P, EARLY_BYTES], U8, name="gs", align_bytes=64)
+        gates_first = keep.tile([P, BANK], F32, name="gates_first")
+        gates_rest = keep.tile([P, SLOTS - BANK], F32, name="gates_rest")
         banks = [ps_t.tile([P, BANK], F32, name=f"bank{b}") for b in range(3)]
         windows = [keep.tile([P, SLOTS], F32, name=f"window{d}") for d in range(PAIRS)]
 
@@ -67,9 +72,12 @@ def tile_moe_mhm_relu2_kernel(
             xw[:].rearrange("p (o t) -> p o t", o=HEADS),
             x_words.rearrange("o p t d -> p o (t d)").bitcast(I32),
         )
-        nc.gpsimd.dma_start(ww[:].bitcast(I32), w_words.rearrange("e s p b -> p (e s) b").bitcast(I32))
+        w_rows = w_words.rearrange("e s p b -> p (e s) b").bitcast(I32)
+        nc.gpsimd.dma_start(ww_first[:].bitcast(I32), w_rows[:, 0:FIRST_EXPERTS])
         make_identity(nc, ident[:])
-        nc.gpsimd.memset(gate_rows[:], 0.0)
+        nc.gpsimd.dma_start(gates_first[:], gate[:, 0:BANK])
+        nc.gpsimd.dma_start(ww_rest[:].bitcast(I32), w_rows[:, FIRST_EXPERTS:EXPERTS])
+        nc.gpsimd.dma_start(gates_rest[:], gate[:, BANK:SLOTS])
         xs_rows = x_scales.bitcast(I32)
         xs_view = xs[:].bitcast(I32).rearrange("p (o t) -> p o t", o=HEADS)
         for q in range(4):
@@ -82,15 +90,13 @@ def tile_moe_mhm_relu2_kernel(
         def listed(j0, j1):
             return offsets[:, j0 // 16 : j1 // 16]
 
-        for sort, j0, j1 in GATHERS:
-            if sort == "bytes":
-                nc.vector.tensor_copy(gs[:, j0:j1], xs[:].indirect(listed(j0, j1)))
-            else:
-                nc.vector.tensor_copy(gw[:, j0:j1], xw[:].bitcast(U32).indirect(listed(j0, j1)))
 
-        nc.sync.dma_start(gate_rows[0:TILES, :], gate[0:1, :].rearrange("r (s j) -> (r s) j", j=P))
-        nc.tensor.transpose(banks[2][:, 0:P], gate_rows[:], ident[:])
-        nc.scalar.copy(gate_cols[:], banks[2][:, 0:TILES])
+        nc.vector.tensor_copy(gs[:], xs[:].indirect(listed(0, EARLY_BYTES)))
+        nc.vector.tensor_copy(gw_first[:], xw[:].bitcast(U32).indirect(listed(0, CAP)))
+        for j0, j1 in ((CAP, BANK), (BANK, SLOTS // 2), (SLOTS // 2, SLOTS)):
+            nc.vector.tensor_copy(gw[:, j0 - CAP : j1 - CAP], xw[:].bitcast(U32).indirect(listed(j0, j1)))
+        gs_late = keep.tile([P, SLOTS - EARLY_BYTES], U8, name="gw_first", align_bytes=64)
+        nc.vector.tensor_copy(gs_late[:], xs[:].indirect(listed(EARLY_BYTES, SLOTS)))
 
         def product(s):
             e = s * P // CAP
@@ -98,50 +104,54 @@ def tile_moe_mhm_relu2_kernel(
             v = ps_y.tile([P, WIDTH], F32, name="v")
             nc.tensor.matmul_mx(
                 out=v[:],
-                lhsT=gw[:, slots].bitcast(FP8X4),
-                lhsT_scale=gs[:, slots],
-                rhs=ww[:, e, :].bitcast(FP4X4),
+                lhsT=(gw_first[:, slots] if e == 0 else gw[:, s * P - CAP : (s + 1) * P - CAP]).bitcast(FP8X4),
+                lhsT_scale=gs[:, slots] if s * P < EARLY_BYTES else gs_late[:, s * P - EARLY_BYTES : (s + 1) * P - EARLY_BYTES],
+                rhs=(ww_first[:, e, :] if e < FIRST_EXPERTS else ww_rest[:, e - FIRST_EXPERTS, :]).bitcast(FP4X4),
                 rhs_scale=ws[:, e * WIDTH : (e + 1) * WIDTH],
                 start=True,
                 stop=True,
             )
-            nc.scalar.activation(
-                r[:, s].rearrange("j u (p e) -> j u p e", e=PAIRS),
-                v[:].rearrange("j (p u e) -> j u p e", u=PAIRS, e=PAIRS),
-                ACT.Relu,
-            )
+            r = keep.tile([P, PACK, P], F32, name=f"r{s}", align_bytes=64)
+            nc.scalar.activation(r[:], v[:].rearrange("j (p d) -> j d p", d=PACK), ACT.Relu)
+            return r
 
-        multiplied = 0
-        for k, (u, j0, j1) in enumerate(SCATTERS):
-            s0, s1 = j0 // P, j1 // P
-            while multiplied < s1:
-                product(multiplied)
-                multiplied += 1
-            y = keep.tile([P, s1 - s0, HALF], F32, name=f"y{k}")
-            nc.scalar.activation(y[:], r[:, s0:s1, u, :], ACT.Square)
-            banks.append(banks.pop(0))
-            for s in range(s0, s1):
-                pairs = keep.tile([P, HALF], BF16, name=f"pairs{s}_{u}", align_bytes=64)
-                nc.gpsimd.tensor_scalar(pairs[:], y[:, s - s0, :], gate_cols[:, s : s + 1], 0.0, MULT, ADD)
-                nc.tensor.transpose(banks[0][:, (s - s0) * P : (s - s0 + 1) * P], pairs[:].bitcast(F32), ident[:])
-            stage = keep.tile([P, j1 - j0], F32, name=f"stage{k}")
-            nc.scalar.copy(stage[:], banks[0][:, 0 : j1 - j0])
-            nc.vector.tensor_copy(windows[u][:].indirect(listed(j0, j1)), stage[:])
+        pieces = PIECES
+        relu = {}
+        for k, (u, j0, j1) in enumerate(pieces):
+            for ahead in pieces[k : k + 1 + AHEAD]:
+                for s in range(ahead[1] // P, ahead[2] // P):
+                    if s not in relu:
+                        relu[s] = product(s)
+            stage = keep.tile([P, (j1 - j0) * PAIRS], BF16, name=f"stage{k}")
+            unit = P if k < FINE else CAP
+            for a in range(j0, j1, unit):
+                banks.append(banks.pop(0))
+                for s in range(a // P, (a + unit) // P):
+                    for e in range(PAIRS):
+                        col = e * unit + s * P - a
+                        nc.tensor.transpose(banks[0][:, col : col + P], relu[s][:, PAIRS * u + e, :], ident[:])
+                y = keep.tile([P, PAIRS, unit], F32, name=f"y{a // P}_{u}", align_bytes=64)
+                nc.scalar.activation(y[:].rearrange("p e j -> p (e j)"), banks[0][:, 0 : PAIRS * unit], ACT.Square)
+                nc.gpsimd.tensor_tensor(
+                    stage[:, (a - j0) * PAIRS : (a - j0 + unit) * PAIRS].rearrange("p (j e) -> p e j", e=PAIRS),
+                    y[:],
+                    (gates_first[:, a : a + unit] if a < BANK else gates_rest[:, a - BANK : a - BANK + unit]).unsqueeze(1).to_broadcast([P, PAIRS, unit]),
+                    MULT,
+                )
+            nc.vector.tensor_copy(windows[u][:].indirect(listed(j0, j1)), stage[:].bitcast(F32))
 
-        grouped = [
-            keep.tile([P, HEADS, CHUNK, PAIRS], U32, name=f"pairs{LENDERS[h]}_1", align_bytes=64) for h in range(CHUNKS)
-        ]
+        early = keep.tile([P, (CHUNKS - 1) * CHUNK_WORDS], U32, name=f"r{TILES - 1}", align_bytes=64)
+        late = keep.tile([P, CHUNK_WORDS], U32, name=f"y{TILES - 2}_1", align_bytes=64)
+        grouped = [early[:, h * CHUNK_WORDS : (h + 1) * CHUNK_WORDS] for h in range(CHUNKS - 1)] + [late[:]]
 
         def plane(u, h, o0, o1, dtype):
             src = windows[u][:].bitcast(dtype).rearrange("p (o h t) -> p h o t", o=HEADS, h=CHUNKS)
-            dst = grouped[h][:].rearrange("p o t u -> p (o t u)").bitcast(dtype).rearrange("p (o t u) -> p o t u", o=HEADS, u=PAIRS)
+            dst = grouped[h].bitcast(dtype).rearrange("p (o t u) -> p o t u", o=HEADS, u=PAIRS)
             return dst[:, o0:o1, :, u], src[:, h, o0:o1]
 
-        for h in range(CHUNKS):
-            if h < SCALAR_CHUNKS:
-                nc.scalar.copy(*plane(0, h, 0, HEADS, U32))
-            else:
-                nc.gpsimd.tensor_copy(*plane(0, h, 0, HEADS, U32))
+        for h in range(CHUNKS - 1):
+            nc.scalar.copy(*plane(0, h, 0, HEADS, U32))
+        nc.gpsimd.tensor_copy(*plane(0, CHUNKS - 1, 0, HEADS, U32))
 
         mw = keep.tile([P, HEADS, N_OUT], I32, name="ww", align_bytes=64)
         ms = keep.tile([P, N_OUT], U8, name="ws", align_bytes=64)
@@ -151,21 +161,30 @@ def tile_moe_mhm_relu2_kernel(
             nc.sync.dma_start(ms[32 * q : 32 * q + 16, :].bitcast(I32), ms_rows[:, 4 * q : 4 * q + 4, :])
         nc.sync.dma_start(mw[:], wm_words.rearrange("s p n d -> p s (n d)").bitcast(I32))
 
+        for i in range(WARM):
+            nc.tensor.matmul_mx(
+                out=banks[0][:],
+                lhsT=mw[:, 0, 0:P].bitcast(FP8X4),
+                lhsT_scale=ms[:, 0:P],
+                rhs=mw[:, 0, :].bitcast(FP8X4),
+                rhs_scale=ms[:],
+                start=True,
+                stop=True,
+            )
+
+        codes = []
         for h in range(CHUNKS):
             split = VECTOR_HEADS[h]
             if split > 0:
                 nc.vector.tensor_copy(*plane(1, h, 0, split, I32))
             if split < HEADS:
                 nc.scalar.copy(*plane(1, h, split, HEADS, U32))
-
-        codes = []
-        for h in range(CHUNKS):
             cw = keep.tile([P, HEADS, CHUNK], U32, name=f"cw{h}", align_bytes=64)
             cs = keep.tile([P, HEADS, CHUNK], U8, name=f"cs{h}", align_bytes=64)
             nc.vector.quantize_mx(
                 out=cw[:].rearrange("p o t -> p (o t)").bitcast(FP8X4),
                 scales=cs[:].rearrange("p o t -> p (o t)"),
-                in_=grouped[h][:].rearrange("p o t u -> p (o t u)").bitcast(BF16),
+                in_=grouped[h].bitcast(BF16),
             )
             codes.append((cw, cs))
 

@@ -34,9 +34,14 @@ TILES = SLOTS // P
 CHUNK = 128
 CHUNKS = TOKENS // CHUNK
 VECTOR_HEADS = (3, 2, 0, 0)
-VECTOR_OUT = ((0, 0), (1, 0), (3, 2))
-WARM = 0
-HELD = 0
+VECTOR_OUT = ((1, 0), (3, 2))
+WARM = 8
+ROWS = N_OUT // P
+GROUPS = (4, 4, 4, 4)
+WIDTHS = (4, 4, 4, 2)
+STORES = (4, 4, 4, 2)
+MS_SLOT = "ws"
+MW_SLOT = "stage8"
 CHUNK_WORDS = HEADS * CHUNK * PAIRS
 
 
@@ -122,7 +127,7 @@ def tile_moe_mhm_relu2_kernel(
                 for s in range(ahead[1] // P, ahead[2] // P):
                     if s not in relu:
                         relu[s] = product(s)
-            stage = keep.tile([P, (j1 - j0) * PAIRS], BF16, name=f"stage{k}")
+            stage = keep.tile([P, (j1 - j0) * PAIRS], BF16, name=f"stage{k}", align_bytes=64)
             unit = P if k < FINE else CAP
             for a in range(j0, j1, unit):
                 banks.append(banks.pop(0))
@@ -153,8 +158,8 @@ def tile_moe_mhm_relu2_kernel(
             nc.scalar.copy(*plane(0, h, 0, HEADS, U32))
         nc.gpsimd.tensor_copy(*plane(0, CHUNKS - 1, 0, HEADS, U32))
 
-        mw = keep.tile([P, HEADS, N_OUT], I32, name="ww", align_bytes=64)
-        ms = keep.tile([P, N_OUT], U8, name="ws", align_bytes=64)
+        mw = keep.tile([P, HEADS, N_OUT], I32, name=MW_SLOT, align_bytes=64)
+        ms = keep.tile([P, N_OUT], U8, name=MS_SLOT, align_bytes=64)
         nc.gpsimd.memset(ms[:].bitcast(I32), 0)
         ms_rows = wm_scales.bitcast(I32)
         for q in range(4):
@@ -172,43 +177,58 @@ def tile_moe_mhm_relu2_kernel(
                 stop=True,
             )
 
-        codes = []
+        codes = {}
         for h in range(CHUNKS):
             split = VECTOR_HEADS[h]
-            if split > 0:
-                nc.vector.tensor_copy(*plane(1, h, 0, split, I32))
-            if split < HEADS:
-                nc.scalar.copy(*plane(1, h, split, HEADS, U32))
-            cw = keep.tile([P, HEADS, CHUNK], U32, name=f"cw{h}", align_bytes=64)
-            cs = keep.tile([P, HEADS, CHUNK], U8, name=f"cs{h}", align_bytes=64)
-            nc.vector.quantize_mx(
-                out=cw[:].rearrange("p o t -> p (o t)").bitcast(FP8X4),
-                scales=cs[:].rearrange("p o t -> p (o t)"),
-                in_=grouped[h].bitcast(BF16),
+            group = GROUPS[h]
+            for o0 in range(0, HEADS, group):
+                o1 = o0 + group
+                mid = min(max(split, o0), o1)
+                if mid > o0:
+                    nc.vector.tensor_copy(*plane(1, h, o0, mid, I32))
+                if mid < o1:
+                    nc.scalar.copy(*plane(1, h, mid, o1, U32))
+                cw = keep.tile([P, group * CHUNK], U32, name=f"cw{h}_{o0}", align_bytes=64)
+                cs = keep.tile([P, group * CHUNK], U8, name=f"cs{h}_{o0}", align_bytes=64)
+                nc.vector.quantize_mx(
+                    out=cw[:].bitcast(FP8X4),
+                    scales=cs[:],
+                    in_=grouped[h][:, o0 * CHUNK * PAIRS : o1 * CHUNK * PAIRS].bitcast(BF16),
+                )
+                for o in range(o0, o1):
+                    cols = slice((o - o0) * CHUNK, (o - o0 + 1) * CHUNK)
+                    codes[h, o] = (cw[:, cols], cs[:, cols])
+
+        def merge(acc, h, m, o):
+            cols = slice(m * P, (m + 1) * P)
+            nc.tensor.matmul_mx(
+                out=acc,
+                lhsT=mw[:, o, cols].bitcast(FP8X4),
+                lhsT_scale=ms[4 * o :, cols],
+                rhs=codes[h, o][0].bitcast(FP8X4),
+                rhs_scale=codes[h, o][1],
+                start=(o == 0),
+                stop=(o == HEADS - 1),
             )
-            codes.append((cw, cs))
 
         out_view = out.rearrange("(m p) t -> p m t", p=P)
-        for h, (cw, cs) in enumerate(codes):
+        for h in range(CHUNKS):
             tokens = slice(h * CHUNK, (h + 1) * CHUNK)
-            parts = ((0, 2), (2, 4)) if h == CHUNKS - 1 else ((0, 4),)
-            for m0, m1 in parts:
-                acc = ps_y.tile([P, m1 - m0, CHUNK], F32, name="v")
-                for m in range(m0, m1):
-                    cols = slice(m * P, (m + 1) * P)
+            width = WIDTHS[h]
+            accs = [ps_y.tile([P, width, CHUNK], F32, name="v") for m0 in range(0, ROWS, width)]
+            if GROUPS[h] < HEADS:
+                for o in range(HEADS):
+                    for m in range(ROWS):
+                        merge(accs[m][:, 0, :], h, m, o)
+            else:
+                for m in range(ROWS):
                     for o in range(HEADS):
-                        nc.tensor.matmul_mx(
-                            out=acc[:, m - m0, :],
-                            lhsT=mw[:, o, cols].bitcast(FP8X4),
-                            lhsT_scale=ms[4 * o :, cols],
-                            rhs=cw[:, o, :].bitcast(FP8X4),
-                            rhs_scale=cs[:, o, :],
-                            start=(o == 0),
-                            stop=(o == HEADS - 1),
-                        )
-                res = ring.tile([P, m1 - m0, CHUNK], F32, name="res")
-                if (h, m0) in VECTOR_OUT:
-                    nc.vector.tensor_copy(res[:], acc[:])
-                else:
-                    nc.scalar.copy(res[:], acc[:])
-                nc.sync.dma_start(out_view[:, m0:m1, tokens], res[:])
+                        merge(accs[m // width][:, m % width, :], h, m, o)
+            for m0 in range(0, ROWS, STORES[h]):
+                res = ring.tile([P, STORES[h], CHUNK], F32, name="res")
+                for m in range(m0, m0 + STORES[h], width):
+                    if (h, m) in VECTOR_OUT:
+                        nc.vector.tensor_copy(res[:, m - m0 : m - m0 + width], accs[m // width][:])
+                    else:
+                        nc.scalar.copy(res[:, m - m0 : m - m0 + width], accs[m // width][:])
+                nc.sync.dma_start(out_view[:, m0 : m0 + STORES[h], tokens], res[:])

@@ -23,7 +23,7 @@ MULT = mybir.AluOpType.mult
 ADD = mybir.AluOpType.add
 
 EARLY_BYTES = 1536
-PIECES = ((0, 0, 256), (1, 0, 256), (0, 256, 512), (1, 256, 512), (0, 512, 1024), (1, 512, 768), (0, 1024, 1536), (1, 768, 1024), (0, 1536, 2048), (1, 1024, 1536), (1, 1536, 2048))
+PIECES = ((0, 0, 256), (1, 0, 256), (0, 256, 512), (1, 256, 512), (0, 512, 1024), (1, 512, 768), (0, 1024, 1536), (1, 768, 1024), (0, 1536, 2048), (1, 1024, 2048))
 AHEAD = 0
 FINE = 1
 FIRST_EXPERTS = 2
@@ -31,18 +31,16 @@ BANK = 512
 PAIRS = 2
 HALF = WIDTH // PAIRS
 TILES = SLOTS // P
-CHUNK = 128
-CHUNKS = TOKENS // CHUNK
-VECTOR_HEADS = (3, 2, 0, 0)
-VECTOR_OUT = ((1, 0), (3, 2))
+VECTOR_OUT = ((1, 1), (1, 3))
 WARM = 8
 ROWS = N_OUT // P
-GROUPS = (4, 4, 4, 4)
-WIDTHS = (4, 4, 4, 2)
-STORES = (4, 4, 4, 2)
+STORES = (2, 1)
 MS_SLOT = "ws"
 MW_SLOT = "stage8"
-CHUNK_WORDS = HEADS * CHUNK * PAIRS
+SPAN = 256
+UNIT_WORDS = SPAN * PAIRS
+STAGED = (4, 5)
+DIRECT = (0, 1)
 
 
 def tile_moe_mhm_relu2_kernel(
@@ -98,7 +96,7 @@ def tile_moe_mhm_relu2_kernel(
 
         nc.vector.tensor_copy(gs[:], xs[:].indirect(listed(0, EARLY_BYTES)))
         nc.vector.tensor_copy(gw_first[:], xw[:].bitcast(U32).indirect(listed(0, CAP)))
-        for j0, j1 in ((CAP, BANK), (BANK, SLOTS // 2), (SLOTS // 2, SLOTS)):
+        for j0, j1 in ((CAP, BANK), (BANK, SLOTS)):
             nc.vector.tensor_copy(gw[:, j0 - CAP : j1 - CAP], xw[:].bitcast(U32).indirect(listed(j0, j1)))
         gs_late = keep.tile([P, SLOTS - EARLY_BYTES], U8, name="gw_first", align_bytes=64)
         nc.vector.tensor_copy(gs_late[:], xs[:].indirect(listed(EARLY_BYTES, SLOTS)))
@@ -145,18 +143,27 @@ def tile_moe_mhm_relu2_kernel(
                 )
             nc.vector.tensor_copy(windows[u][:].indirect(listed(j0, j1)), stage[:].bitcast(F32))
 
-        early = keep.tile([P, (CHUNKS - 1) * CHUNK_WORDS], U32, name=f"r{TILES - 1}", align_bytes=64)
-        late = keep.tile([P, CHUNK_WORDS], U32, name=f"y{TILES - 2}_1", align_bytes=64)
-        grouped = [early[:, h * CHUNK_WORDS : (h + 1) * CHUNK_WORDS] for h in range(CHUNKS - 1)] + [late[:]]
+        units = [(g, o) for g in range(TOKENS // SPAN) for o in range(HEADS)]
+        staged = [i for i in range(len(units)) if i in STAGED]
+        room = keep.tile([P, (len(units) + len(staged)) * UNIT_WORDS], U32, name=f"r{TILES - 1}", align_bytes=64)
 
-        def plane(u, h, o0, o1, dtype):
-            src = windows[u][:].bitcast(dtype).rearrange("p (o h t) -> p h o t", o=HEADS, h=CHUNKS)
-            dst = grouped[h].bitcast(dtype).rearrange("p (o t u) -> p o t u", o=HEADS, u=PAIRS)
-            return dst[:, o0:o1, :, u], src[:, h, o0:o1]
+        def woven(i, dtype):
+            return room[:, i * UNIT_WORDS : (i + 1) * UNIT_WORDS].bitcast(dtype)
 
-        for h in range(CHUNKS - 1):
-            nc.scalar.copy(*plane(0, h, 0, HEADS, U32))
-        nc.gpsimd.tensor_copy(*plane(0, CHUNKS - 1, 0, HEADS, U32))
+        def apart(i, dtype):
+            return woven(len(units) + staged.index(i), dtype).rearrange("p (u t) -> p u t", u=PAIRS)
+
+        def source(u, i, dtype):
+            g, o = units[i]
+            return windows[u][:, o * TOKENS + g * SPAN : o * TOKENS + (g + 1) * SPAN].bitcast(dtype)
+
+        def target(u, i, dtype):
+            if i in staged:
+                return apart(i, dtype)[:, u, :]
+            return woven(i, dtype).rearrange("p (t u) -> p t u", u=PAIRS)[:, :, u]
+
+        for i in range(len(units)):
+            nc.scalar.copy(target(0, i, U32), source(0, i, U32))
 
         mw = keep.tile([P, HEADS, N_OUT], I32, name=MW_SLOT, align_bytes=64)
         ms = keep.tile([P, N_OUT], U8, name=MS_SLOT, align_bytes=64)
@@ -177,58 +184,43 @@ def tile_moe_mhm_relu2_kernel(
                 stop=True,
             )
 
-        codes = {}
-        for h in range(CHUNKS):
-            split = VECTOR_HEADS[h]
-            group = GROUPS[h]
-            for o0 in range(0, HEADS, group):
-                o1 = o0 + group
-                mid = min(max(split, o0), o1)
-                if mid > o0:
-                    nc.vector.tensor_copy(*plane(1, h, o0, mid, I32))
-                if mid < o1:
-                    nc.scalar.copy(*plane(1, h, mid, o1, U32))
-                cw = keep.tile([P, group * CHUNK], U32, name=f"cw{h}_{o0}", align_bytes=64)
-                cs = keep.tile([P, group * CHUNK], U8, name=f"cs{h}_{o0}", align_bytes=64)
-                nc.vector.quantize_mx(
-                    out=cw[:].bitcast(FP8X4),
-                    scales=cs[:],
-                    in_=grouped[h][:, o0 * CHUNK * PAIRS : o1 * CHUNK * PAIRS].bitcast(BF16),
-                )
-                for o in range(o0, o1):
-                    cols = slice((o - o0) * CHUNK, (o - o0 + 1) * CHUNK)
-                    codes[h, o] = (cw[:, cols], cs[:, cols])
-
-        def merge(acc, h, m, o):
-            cols = slice(m * P, (m + 1) * P)
-            nc.tensor.matmul_mx(
-                out=acc,
-                lhsT=mw[:, o, cols].bitcast(FP8X4),
-                lhsT_scale=ms[4 * o :, cols],
-                rhs=codes[h, o][0].bitcast(FP8X4),
-                rhs_scale=codes[h, o][1],
-                start=(o == 0),
-                stop=(o == HEADS - 1),
-            )
-
-        out_view = out.rearrange("(m p) t -> p m t", p=P)
-        for h in range(CHUNKS):
-            tokens = slice(h * CHUNK, (h + 1) * CHUNK)
-            width = WIDTHS[h]
-            accs = [ps_y.tile([P, width, CHUNK], F32, name="v") for m0 in range(0, ROWS, width)]
-            if GROUPS[h] < HEADS:
-                for o in range(HEADS):
-                    for m in range(ROWS):
-                        merge(accs[m][:, 0, :], h, m, o)
+        codes = []
+        for i in range(len(units)):
+            if i in DIRECT:
+                nc.vector.tensor_copy(target(1, i, I32), source(1, i, I32))
             else:
-                for m in range(ROWS):
-                    for o in range(HEADS):
-                        merge(accs[m // width][:, m % width, :], h, m, o)
-            for m0 in range(0, ROWS, STORES[h]):
-                res = ring.tile([P, STORES[h], CHUNK], F32, name="res")
-                for m in range(m0, m0 + STORES[h], width):
-                    if (h, m) in VECTOR_OUT:
-                        nc.vector.tensor_copy(res[:, m - m0 : m - m0 + width], accs[m // width][:])
+                nc.scalar.copy(target(1, i, U32), source(1, i, U32))
+            if i in staged:
+                nc.vector.tensor_copy(woven(i, I32).rearrange("p (t u) -> p t u", u=PAIRS), apart(i, I32).rearrange("p u t -> p t u"))
+            cw = keep.tile([P, SPAN], U32, name=f"cw{i}", align_bytes=64)
+            cs = keep.tile([P, SPAN], U8, name=f"cs{i}", align_bytes=64)
+            nc.vector.quantize_mx(out=cw[:].bitcast(FP8X4), scales=cs[:], in_=woven(i, BF16))
+            codes.append((cw, cs))
+
+        free = [ps_y.tile([P, BANK], F32, name="v") for b in range(5)] + banks
+        for g in range(TOKENS // SPAN):
+            accs = free[g * ROWS : (g + 1) * ROWS]
+            last = g == TOKENS // SPAN - 1
+            order = [(o, m) for o in range(HEADS - (2 if last else 0)) for m in range(ROWS)]
+            if last:
+                order.extend((o, m) for m in range(ROWS) for o in range(HEADS - 2, HEADS))
+            for o, m in order:
+                cols = slice(m * P, (m + 1) * P)
+                cw, cs = codes[g * HEADS + o]
+                nc.tensor.matmul_mx(
+                    out=accs[m][:, 0:SPAN],
+                    lhsT=mw[:, o, cols].bitcast(FP8X4),
+                    lhsT_scale=ms[4 * o :, cols],
+                    rhs=cw[:].bitcast(FP8X4),
+                    rhs_scale=cs[:],
+                    start=(o == 0),
+                    stop=(o == HEADS - 1),
+                )
+            for m0 in range(0, ROWS, STORES[g]):
+                res = ring.tile([P, STORES[g], SPAN], F32, name="res")
+                for m in range(m0, m0 + STORES[g]):
+                    if (g, m) in VECTOR_OUT:
+                        nc.vector.tensor_copy(res[:, m - m0], accs[m][:, 0:SPAN])
                     else:
-                        nc.scalar.copy(res[:, m - m0 : m - m0 + width], accs[m // width][:])
-                nc.sync.dma_start(out_view[:, m0 : m0 + STORES[h], tokens], res[:])
+                        nc.scalar.copy(res[:, m - m0], accs[m][:, 0:SPAN])
+                nc.sync.dma_start(out.rearrange("(m p) t -> p m t", p=P)[:, m0 : m0 + STORES[g], g * SPAN : (g + 1) * SPAN], res[:])

@@ -58,7 +58,8 @@ def tile_moe_mhm_relu2_kernel(
         xs = keep.tile([P, SLOTS], U8, name="xs", align_bytes=64)
         ww_first = keep.tile([P, FIRST_EXPERTS, 2 * WIDTH], U8, name="ww_first", align_bytes=64)
         ww_rest = keep.tile([P, EXPERTS - FIRST_EXPERTS, 2 * WIDTH], U8, name="ww", align_bytes=64)
-        ws = keep.tile([P, EXPERTS * WIDTH], U8, name="ws", align_bytes=64)
+        ws_first = keep.tile([P, FIRST_EXPERTS * WIDTH], U8, name="ws_first", align_bytes=64)
+        ws_rest = keep.tile([P, (EXPERTS - FIRST_EXPERTS) * WIDTH], U8, name="ws", align_bytes=64)
         ident = keep.tile([P, P], F32, name="ident")
         gw_first = keep.tile([P, CAP], U32, name="gw_first", align_bytes=64)
         gw = keep.tile([P, SLOTS - CAP], U32, name="gw", align_bytes=64)
@@ -69,16 +70,17 @@ def tile_moe_mhm_relu2_kernel(
         windows = [keep.tile([P, SLOTS], F32, name=f"window{d}") for d in range(PAIRS)]
 
         nc.gpsimd.memset(xs[:].bitcast(I32), 0)
-        nc.vector.memset(ws[:].bitcast(I32), 0)
         nc.sync.dma_start(offsets[:], offs)
         nc.gpsimd.dma_start(
             xw[:].rearrange("p (o t) -> p o t", o=HEADS),
             x_words.rearrange("o p t d -> p o (t d)").bitcast(I32),
         )
+        nc.gpsimd.memset(ws_first[:].bitcast(I32), 0)
         w_rows = w_words.rearrange("e s p b -> p (e s) b").bitcast(I32)
         nc.gpsimd.dma_start(ww_first[:].bitcast(I32), w_rows[:, 0:FIRST_EXPERTS])
         make_identity(nc, ident[:])
         nc.gpsimd.dma_start(gates_first[:], gate[:, 0:BANK])
+        nc.gpsimd.memset(ws_rest[:].bitcast(I32), 0)
         nc.gpsimd.dma_start(ww_rest[:].bitcast(I32), w_rows[:, FIRST_EXPERTS:EXPERTS])
         nc.gpsimd.dma_start(gates_rest[:], gate[:, BANK:SLOTS])
         xs_rows = x_scales.bitcast(I32)
@@ -86,9 +88,10 @@ def tile_moe_mhm_relu2_kernel(
         for q in range(4):
             nc.sync.dma_start(xs_view[32 * q : 32 * q + 4], xs_rows[:, 4 * q : 4 * q + 4, :].rearrange("o r t -> r o t"))
         ws_rows = w_scales.rearrange("e s b l -> (e s) b l").bitcast(I32)
-        ws_view = ws[:].bitcast(I32).rearrange("p (e l) -> p e l", e=EXPERTS)
-        for q in range(4):
-            nc.sync.dma_start(ws_view[32 * q : 32 * q + 4], ws_rows[:, 4 * q : 4 * q + 4, :].rearrange("e r l -> r e l"))
+        for tile, e0, e1 in ((ws_first, 0, FIRST_EXPERTS), (ws_rest, FIRST_EXPERTS, EXPERTS)):
+            view = tile[:].bitcast(I32).rearrange("p (e l) -> p e l", e=e1 - e0)
+            for q in range(4):
+                nc.sync.dma_start(view[32 * q : 32 * q + 4], ws_rows[e0:e1, 4 * q : 4 * q + 4, :].rearrange("e r l -> r e l"))
 
         def listed(j0, j1):
             return offsets[:, j0 // 16 : j1 // 16]
@@ -110,7 +113,7 @@ def tile_moe_mhm_relu2_kernel(
                 lhsT=(gw_first[:, slots] if e == 0 else gw[:, s * P - CAP : (s + 1) * P - CAP]).bitcast(FP8X4),
                 lhsT_scale=gs[:, slots] if s * P < EARLY_BYTES else gs_late[:, s * P - EARLY_BYTES : (s + 1) * P - EARLY_BYTES],
                 rhs=(ww_first[:, e, :] if e < FIRST_EXPERTS else ww_rest[:, e - FIRST_EXPERTS, :]).bitcast(FP4X4),
-                rhs_scale=ws[:, e * WIDTH : (e + 1) * WIDTH],
+                rhs_scale=ws_first[:, e * WIDTH : (e + 1) * WIDTH] if e < FIRST_EXPERTS else ws_rest[:, (e - FIRST_EXPERTS) * WIDTH : (e - FIRST_EXPERTS + 1) * WIDTH],
                 start=True,
                 stop=True,
             )

@@ -22,7 +22,7 @@ ACT = mybir.ActivationFunctionType
 MULT = mybir.AluOpType.mult
 ADD = mybir.AluOpType.add
 
-EARLY_BYTES = 1536
+EARLY_BYTES = 1280
 PIECES = ((0, 0, 256), (1, 0, 256), (0, 256, 512), (1, 256, 512), (0, 512, 1024), (1, 512, 768), (0, 1024, 1536), (1, 768, 1024), (0, 1536, 2048), (1, 1024, 2048))
 AHEAD = 0
 FINE = 1
@@ -69,16 +69,16 @@ def tile_moe_mhm_relu2_kernel(
         banks = [ps_t.tile([P, BANK], F32, name=f"bank{b}") for b in range(3)]
         windows = [keep.tile([P, SLOTS], F32, name=f"window{d}") for d in range(PAIRS)]
 
-        nc.gpsimd.memset(xs[:].bitcast(I32), 0)
+        nc.vector.memset(xs[:].bitcast(I32), 0)
         nc.sync.dma_start(offsets[:], offs)
         nc.gpsimd.dma_start(
             xw[:].rearrange("p (o t) -> p o t", o=HEADS),
             x_words.rearrange("o p t d -> p o (t d)").bitcast(I32),
         )
-        nc.gpsimd.memset(ws_first[:].bitcast(I32), 0)
         w_rows = w_words.rearrange("e s p b -> p (e s) b").bitcast(I32)
         nc.gpsimd.dma_start(ww_first[:].bitcast(I32), w_rows[:, 0:FIRST_EXPERTS])
         make_identity(nc, ident[:])
+        nc.gpsimd.memset(ws_first[:].bitcast(I32), 0)
         nc.gpsimd.dma_start(gates_first[:], gate[:, 0:BANK])
         nc.gpsimd.memset(ws_rest[:].bitcast(I32), 0)
         nc.gpsimd.dma_start(ww_rest[:].bitcast(I32), w_rows[:, FIRST_EXPERTS:EXPERTS])
@@ -86,7 +86,7 @@ def tile_moe_mhm_relu2_kernel(
         xs_rows = x_scales.bitcast(I32)
         xs_view = xs[:].bitcast(I32).rearrange("p (o t) -> p o t", o=HEADS)
         for q in range(4):
-            nc.sync.dma_start(xs_view[32 * q : 32 * q + 4], xs_rows[:, 4 * q : 4 * q + 4, :].rearrange("o r t -> r o t"))
+            (nc.sync, nc.scalar)[q % 2].dma_start(xs_view[32 * q : 32 * q + 4], xs_rows[:, 4 * q : 4 * q + 4, :].rearrange("o r t -> r o t"))
         ws_rows = w_scales.rearrange("e s b l -> (e s) b l").bitcast(I32)
         for tile, e0, e1 in ((ws_first, 0, FIRST_EXPERTS), (ws_rest, FIRST_EXPERTS, EXPERTS)):
             view = tile[:].bitcast(I32).rearrange("p (e l) -> p e l", e=e1 - e0)

@@ -32,7 +32,7 @@ PAIRS = 2
 HALF = WIDTH // PAIRS
 TILES = SLOTS // P
 VECTOR_OUT = ((1, 1), (1, 3))
-WARM = 8
+WARM = 6
 ROWS = N_OUT // P
 STORES = (2, 1)
 MS_SLOT = "ws"

@@ -85,13 +85,13 @@ def tile_moe_mhm_relu2_kernel(
         nc.gpsimd.dma_start(gates_rest[:], gate[:, BANK:SLOTS])
         xs_rows = x_scales.bitcast(I32)
         xs_view = xs[:].bitcast(I32).rearrange("p (o t) -> p o t", o=HEADS)
-        for q in range(4):
-            (nc.sync, nc.scalar)[q % 2].dma_start(xs_view[32 * q : 32 * q + 4], xs_rows[:, 4 * q : 4 * q + 4, :].rearrange("o r t -> r o t"))
+        for r in range(4):
+            (nc.sync, nc.scalar)[r % 2].dma_start(xs_view[r:P:32], xs_rows.rearrange("o (q r) t -> r q o t", r=4)[r])
         ws_rows = w_scales.rearrange("e s b l -> (e s) b l").bitcast(I32)
         for tile, e0, e1 in ((ws_first, 0, FIRST_EXPERTS), (ws_rest, FIRST_EXPERTS, EXPERTS)):
             view = tile[:].bitcast(I32).rearrange("p (e l) -> p e l", e=e1 - e0)
-            for q in range(4):
-                nc.sync.dma_start(view[32 * q : 32 * q + 4], ws_rows[e0:e1, 4 * q : 4 * q + 4, :].rearrange("e r l -> r e l"))
+            for r in range(4):
+                nc.sync.dma_start(view[r:P:32], ws_rows[e0:e1].rearrange("e (q r) l -> r q e l", r=4)[r])
 
         def listed(j0, j1):
             return offsets[:, j0 // 16 : j1 // 16]

@@ -24,7 +24,7 @@ ADD = mybir.AluOpType.add
 
 EARLY_BYTES = 1280
 PIECES = ((0, 0, 256), (1, 0, 256), (0, 256, 512), (1, 256, 512), (0, 512, 1024), (1, 512, 768), (0, 1024, 1536), (1, 768, 1024), (0, 1536, 2048), (1, 1024, 2048))
-AHEAD = 0
+LEAD = 3
 FINE = 1
 FIRST_EXPERTS = 2
 BANK = 512
@@ -123,14 +123,16 @@ def tile_moe_mhm_relu2_kernel(
 
         pieces = PIECES
         relu = {}
+        ends = [a + CAP for u, j0, j1 in pieces for a in range(j0, j1, CAP)] + [0]
+        step = 0
         for k, (u, j0, j1) in enumerate(pieces):
-            for ahead in pieces[k : k + 1 + AHEAD]:
-                for s in range(ahead[1] // P, ahead[2] // P):
-                    if s not in relu:
-                        relu[s] = product(s)
             stage = keep.tile([P, (j1 - j0) * PAIRS], BF16, name=f"stage{k}", align_bytes=64)
             unit = P if k < FINE else CAP
             for a in range(j0, j1, unit):
+                if a % CAP == 0:
+                    step = step + 1
+                    for s in range(len(relu), min(TILES, max(LEAD, len(relu) + 1, ends[step] // P))):
+                        relu[s] = product(s)
                 banks.append(banks.pop(0))
                 for s in range(a // P, (a + unit) // P):
                     for e in range(PAIRS):

@@ -70,6 +70,7 @@ def tile_moe_mhm_relu2_kernel(
         windows = [keep.tile([P, SLOTS], F32, name=f"window{d}") for d in range(PAIRS)]
 
         nc.vector.memset(xs[:].bitcast(I32), 0)
+        nc.vector.memset(ws_first[:].bitcast(I32), 0)
         nc.sync.dma_start(offsets[:], offs)
         nc.gpsimd.dma_start(
             xw[:].rearrange("p (o t) -> p o t", o=HEADS),
@@ -78,7 +79,6 @@ def tile_moe_mhm_relu2_kernel(
         w_rows = w_words.rearrange("e s p b -> p (e s) b").bitcast(I32)
         nc.gpsimd.dma_start(ww_first[:].bitcast(I32), w_rows[:, 0:FIRST_EXPERTS])
         make_identity(nc, ident[:])
-        nc.gpsimd.memset(ws_first[:].bitcast(I32), 0)
         nc.gpsimd.dma_start(gates_first[:], gate[:, 0:BANK])
         nc.gpsimd.memset(ws_rest[:].bitcast(I32), 0)
         nc.gpsimd.dma_start(ww_rest[:].bitcast(I32), w_rows[:, FIRST_EXPERTS:EXPERTS])
@@ -91,7 +91,7 @@ def tile_moe_mhm_relu2_kernel(
         for tile, e0, e1 in ((ws_first, 0, FIRST_EXPERTS), (ws_rest, FIRST_EXPERTS, EXPERTS)):
             view = tile[:].bitcast(I32).rearrange("p (e l) -> p e l", e=e1 - e0)
             for r in range(4):
-                nc.sync.dma_start(view[r:P:32], ws_rows[e0:e1].rearrange("e (q r) l -> r q e l", r=4)[r])
+                (nc.sync, nc.scalar)[r == 1 and e0 == 0].dma_start(view[r:P:32], ws_rows[e0:e1].rearrange("e (q r) l -> r q e l", r=4)[r])
 
         def listed(j0, j1):
             return offsets[:, j0 // 16 : j1 // 16]

@@ -34,12 +34,13 @@ TILES = SLOTS // P
 VECTOR_OUT = ((1, 1), (1, 3))
 WARM = 6
 ROWS = N_OUT // P
-STORES = (2, 1)
+STORES = (((0, 1), (1, 2), (2, 3), (3, 4)), ((0, 1), (1, 2), (2, 3), (3, 4)))
 MS_SLOT = "ws"
 MW_SLOT = "stage8"
 SPAN = 256
 UNIT_WORDS = SPAN * PAIRS
-STAGED = (4, 5)
+STAGED = (4, 5, 7)
+BY_DMA = (7,)
 DIRECT = (0, 1)
 
 
@@ -49,7 +50,7 @@ def tile_moe_mhm_relu2_kernel(
     nc = tc.nc
     with ExitStack() as ctx:
         keep = ctx.enter_context(tc.tile_pool(name="keep", bufs=1))
-        ring = ctx.enter_context(tc.tile_pool(name="ring", bufs=6))
+        ring = ctx.enter_context(tc.tile_pool(name="ring", bufs=8))
         ps_y = ctx.enter_context(tc.psum_pool(name="ps_y", bufs=5))
         ps_t = ctx.enter_context(tc.psum_pool(name="ps_t", bufs=1))
 
@@ -149,22 +150,19 @@ def tile_moe_mhm_relu2_kernel(
             nc.vector.tensor_copy(windows[u][:].indirect(listed(j0, j1)), stage[:].bitcast(F32))
 
         units = [(g, o) for g in range(TOKENS // SPAN) for o in range(HEADS)]
-        staged = [i for i in range(len(units)) if i in STAGED]
-        room = keep.tile([P, (len(units) + len(staged)) * UNIT_WORDS], U32, name=f"r{TILES - 1}", align_bytes=64)
+        room = keep.tile([P, len(units) * UNIT_WORDS], U32, name=f"r{TILES - 1}", align_bytes=64)
+        aparts = {i: keep.tile([P, PAIRS, SPAN], U32, name=f"r{TILES - 2 - n}", align_bytes=64) for n, i in enumerate(STAGED)}
 
         def woven(i, dtype):
             return room[:, i * UNIT_WORDS : (i + 1) * UNIT_WORDS].bitcast(dtype)
-
-        def apart(i, dtype):
-            return woven(len(units) + staged.index(i), dtype).rearrange("p (u t) -> p u t", u=PAIRS)
 
         def source(u, i, dtype):
             g, o = units[i]
             return windows[u][:, o * TOKENS + g * SPAN : o * TOKENS + (g + 1) * SPAN].bitcast(dtype)
 
         def target(u, i, dtype):
-            if i in staged:
-                return apart(i, dtype)[:, u, :]
+            if i in STAGED:
+                return aparts[i][:].bitcast(dtype)[:, u, :]
             return woven(i, dtype).rearrange("p (t u) -> p t u", u=PAIRS)[:, :, u]
 
         for i in range(len(units)):
@@ -176,7 +174,9 @@ def tile_moe_mhm_relu2_kernel(
         ms_rows = wm_scales.bitcast(I32)
         for q in range(4):
             nc.sync.dma_start(ms[32 * q : 32 * q + 16, :].bitcast(I32), ms_rows[:, 4 * q : 4 * q + 4, :])
-        nc.sync.dma_start(mw[:], wm_words.rearrange("s p n d -> p s (n d)").bitcast(I32))
+        mw_rows = wm_words.rearrange("s p n d -> p s (n d)").bitcast(I32)
+        for o in reversed(range(HEADS)):
+            nc.sync.dma_start(mw[:, o], mw_rows[:, o])
 
         for i in range(WARM):
             nc.tensor.matmul_mx(
@@ -189,14 +189,17 @@ def tile_moe_mhm_relu2_kernel(
                 stop=True,
             )
 
+        for i in BY_DMA:
+            nc.sync.dma_start(target(1, i, I32), source(1, i, I32))
+
         codes = []
         for i in range(len(units)):
             if i in DIRECT:
                 nc.vector.tensor_copy(target(1, i, I32), source(1, i, I32))
-            else:
+            elif i not in BY_DMA:
                 nc.scalar.copy(target(1, i, U32), source(1, i, U32))
-            if i in staged:
-                nc.vector.tensor_copy(woven(i, I32).rearrange("p (t u) -> p t u", u=PAIRS), apart(i, I32).rearrange("p u t -> p t u"))
+            if i in STAGED:
+                nc.vector.tensor_copy(woven(i, I32).rearrange("p (t u) -> p t u", u=PAIRS), aparts[i][:].bitcast(I32).rearrange("p u t -> p t u"))
             cw = keep.tile([P, SPAN], U32, name=f"cw{i}", align_bytes=64)
             cs = keep.tile([P, SPAN], U8, name=f"cs{i}", align_bytes=64)
             nc.vector.quantize_mx(out=cw[:].bitcast(FP8X4), scales=cs[:], in_=woven(i, BF16))
@@ -205,10 +208,8 @@ def tile_moe_mhm_relu2_kernel(
         free = [ps_y.tile([P, BANK], F32, name="v") for b in range(5)] + banks
         for g in range(TOKENS // SPAN):
             accs = free[g * ROWS : (g + 1) * ROWS]
-            last = g == TOKENS // SPAN - 1
-            order = [(o, m) for o in range(HEADS - (2 if last else 0)) for m in range(ROWS)]
-            if last:
-                order.extend((o, m) for m in range(ROWS) for o in range(HEADS - 2, HEADS))
+            order = [(o, m) for o in range(HEADS - 2) for m in range(ROWS)]
+            order.extend((o, m) for m in range(ROWS) for o in range(HEADS - 2, HEADS))
             for o, m in order:
                 cols = slice(m * P, (m + 1) * P)
                 cw, cs = codes[g * HEADS + o]
@@ -221,11 +222,11 @@ def tile_moe_mhm_relu2_kernel(
                     start=(o == 0),
                     stop=(o == HEADS - 1),
                 )
-            for m0 in range(0, ROWS, STORES[g]):
-                res = ring.tile([P, STORES[g], SPAN], F32, name="res")
-                for m in range(m0, m0 + STORES[g]):
+            for m0, m1 in STORES[g]:
+                res = ring.tile([P, m1 - m0, SPAN], F32, name="res")
+                for m in range(m0, m1):
                     if (g, m) in VECTOR_OUT:
                         nc.vector.tensor_copy(res[:, m - m0], accs[m][:, 0:SPAN])
                     else:
                         nc.scalar.copy(res[:, m - m0], accs[m][:, 0:SPAN])
-                nc.sync.dma_start(out.rearrange("(m p) t -> p m t", p=P)[:, m0 : m0 + STORES[g], g * SPAN : (g + 1) * SPAN], res[:])
+                nc.sync.dma_start(out.rearrange("(m p) t -> p m t", p=P)[:, m0:m1, g * SPAN : (g + 1) * SPAN], res[:])

@@ -22,7 +22,7 @@ ACT = mybir.ActivationFunctionType
 MULT = mybir.AluOpType.mult
 ADD = mybir.AluOpType.add
 
-EARLY_BYTES = 1280
+EARLY_BYTES = 1408
 PIECES = ((0, 0, 256), (1, 0, 256), (0, 256, 512), (1, 256, 512), (0, 512, 1024), (1, 512, 768), (0, 1024, 1536), (1, 768, 1024), (0, 1536, 2048), (1, 1024, 2048))
 LEAD = 3
 FINE = 1

@@ -32,7 +32,7 @@ PAIRS = 2
 HALF = WIDTH // PAIRS
 TILES = SLOTS // P
 VECTOR_OUT = ((1, 1), (1, 3))
-WARM = 6
+WARM = 3
 ROWS = N_OUT // P
 STORES = (((0, 1), (1, 2), (2, 3), (3, 4)), ((0, 1), (1, 2), (2, 3), (3, 4)))
 MS_SLOT = "ws"

@@ -23,7 +23,7 @@ MULT = mybir.AluOpType.mult
 ADD = mybir.AluOpType.add
 
 EARLY_BYTES = 1408
-PIECES = ((0, 0, 256), (1, 0, 256), (0, 256, 512), (1, 256, 512), (0, 512, 1024), (1, 512, 768), (0, 1024, 1536), (1, 768, 1024), (0, 1536, 2048), (1, 1024, 2048))
+PIECES = ((0, 0, 256), (1, 0, 256), (0, 256, 512), (1, 256, 512), (0, 512, 1024), (1, 512, 768), (0, 1024, 1536), (1, 768, 1152), (0, 1536, 2048), (1, 1152, 2048))
 LEAD = 3
 FINE = 1
 FIRST_EXPERTS = 2
@@ -124,12 +124,13 @@ def tile_moe_mhm_relu2_kernel(
 
         pieces = PIECES
         relu = {}
-        ends = [a + CAP for u, j0, j1 in pieces for a in range(j0, j1, CAP)] + [0]
+        ends = [a + CAP for u, j0, j1 in pieces for a in range(j0, j1, P) if a % CAP == 0] + [0]
         step = 0
         for k, (u, j0, j1) in enumerate(pieces):
             stage = keep.tile([P, (j1 - j0) * PAIRS], BF16, name=f"stage{k}", align_bytes=64)
-            unit = P if k < FINE else CAP
-            for a in range(j0, j1, unit):
+            starts = [a for a in range(j0, j1, P) if k < FINE or a % CAP == 0 or a == j0]
+            for a, b in zip(starts, starts[1:] + [j1]):
+                unit = b - a
                 if a % CAP == 0:
                     step = step + 1
                     for s in range(len(relu), min(TILES, max(LEAD, len(relu) + 1, ends[step] // P))):

from contextlib import ExitStack

import concourse.mybir as mybir
from concourse.masks import make_identity

HEADS, TOKENS, EXPERTS, CAP, WIDTH, N_OUT = 4, 512, 8, 256, 512, 512
SLOTS = EXPERTS * CAP
P = 128
PACK = 4
FLOPS = 2 * WIDTH * WIDTH * SLOTS + 2 * HEADS * WIDTH * N_OUT * TOKENS
BYTES = 4 * 1048576 + 524288 + 2 * 32768 + 65536 + 32768

F32 = mybir.dt.float32
BF16 = mybir.dt.bfloat16
I32 = mybir.dt.int32
U32 = mybir.dt.uint32
U16 = mybir.dt.uint16
U8 = mybir.dt.uint8
FP8X4 = mybir.dt.float8_e4m3fn_x4
FP4X4 = mybir.dt.float4_e2m1fn_x4
ACT = mybir.ActivationFunctionType
MULT = mybir.AluOpType.mult
ADD = mybir.AluOpType.add

EARLY_BYTES = 1408
PIECES = ((0, 0, 256), (1, 0, 256), (0, 256, 512), (1, 256, 512), (0, 512, 1024), (1, 512, 768), (0, 1024, 1536), (1, 768, 1152), (0, 1536, 2048), (1, 1152, 2048))
LEAD = 3
FINE = 1
FIRST_EXPERTS = 2
BANK = 512
PAIRS = 2
HALF = WIDTH // PAIRS
TILES = SLOTS // P
VECTOR_OUT = ((1, 1), (1, 3))
WARM = 3
ROWS = N_OUT // P
STORES = (((0, 1), (1, 2), (2, 3), (3, 4)), ((0, 1), (1, 2), (2, 3), (3, 4)))
MS_SLOT = "ws"
MW_SLOT = "stage8"
SPAN = 256
UNIT_WORDS = SPAN * PAIRS
STAGED = (4, 5, 7)
BY_DMA = (7,)
DIRECT = (0, 1)


def tile_moe_mhm_relu2_kernel(
    tc, x_words, x_scales, w_words, w_scales, wm_words, wm_scales, gate, offs, out
):
    nc = tc.nc
    with ExitStack() as ctx:
        keep = ctx.enter_context(tc.tile_pool(name="keep", bufs=1))
        ring = ctx.enter_context(tc.tile_pool(name="ring", bufs=8))
        ps_y = ctx.enter_context(tc.psum_pool(name="ps_y", bufs=5))
        ps_t = ctx.enter_context(tc.psum_pool(name="ps_t", bufs=1))

        offsets = keep.tile([P, SLOTS // 16], U16, name="offsets")
        xw = keep.tile([P, SLOTS], I32, name="xw", align_bytes=64)
        xs = keep.tile([P, SLOTS], U8, name="xs", align_bytes=64)
        ww_first = keep.tile([P, FIRST_EXPERTS, 2 * WIDTH], U8, name="ww_first", align_bytes=64)
        ww_rest = keep.tile([P, EXPERTS - FIRST_EXPERTS, 2 * WIDTH], U8, name="ww", align_bytes=64)
        ws_first = keep.tile([P, FIRST_EXPERTS * WIDTH], U8, name="ws_first", align_bytes=64)
        ws_rest = keep.tile([P, (EXPERTS - FIRST_EXPERTS) * WIDTH], U8, name="ws", align_bytes=64)
        ident = keep.tile([P, P], F32, name="ident")
        gw_first = keep.tile([P, CAP], U32, name="gw_first", align_bytes=64)
        gw = keep.tile([P, SLOTS - CAP], U32, name="gw", align_bytes=64)
        gs = keep.tile([P, EARLY_BYTES], U8, name="gs", align_bytes=64)
        gates_first = keep.tile([P, BANK], F32, name="gates_first")
        gates_rest = keep.tile([P, SLOTS - BANK], F32, name="gates_rest")
        banks = [ps_t.tile([P, BANK], F32, name=f"bank{b}") for b in range(3)]
        windows = [keep.tile([P, SLOTS], F32, name=f"window{d}") for d in range(PAIRS)]

        nc.vector.memset(xs[:].bitcast(I32), 0)
        nc.vector.memset(ws_first[:].bitcast(I32), 0)
        nc.sync.dma_start(offsets[:], offs)
        nc.gpsimd.dma_start(
            xw[:].rearrange("p (o t) -> p o t", o=HEADS),
            x_words.rearrange("o p t d -> p o (t d)").bitcast(I32),
        )
        w_rows = w_words.rearrange("e s p b -> p (e s) b").bitcast(I32)
        nc.gpsimd.dma_start(ww_first[:].bitcast(I32), w_rows[:, 0:FIRST_EXPERTS])
        make_identity(nc, ident[:])
        nc.gpsimd.dma_start(gates_first[:], gate[:, 0:BANK])
        nc.gpsimd.memset(ws_rest[:].bitcast(I32), 0)
        nc.gpsimd.dma_start(ww_rest[:].bitcast(I32), w_rows[:, FIRST_EXPERTS:EXPERTS])
        nc.gpsimd.dma_start(gates_rest[:], gate[:, BANK:SLOTS])
        xs_rows = x_scales.bitcast(I32)
        xs_view = xs[:].bitcast(I32).rearrange("p (o t) -> p o t", o=HEADS)
        for r in range(4):
            (nc.sync, nc.scalar)[r % 2].dma_start(xs_view[r:P:32], xs_rows.rearrange("o (q r) t -> r q o t", r=4)[r])
        ws_rows = w_scales.rearrange("e s b l -> (e s) b l").bitcast(I32)
        for tile, e0, e1 in ((ws_first, 0, FIRST_EXPERTS), (ws_rest, FIRST_EXPERTS, EXPERTS)):
            view = tile[:].bitcast(I32).rearrange("p (e l) -> p e l", e=e1 - e0)
            for r in range(4):
                (nc.sync, nc.scalar)[r == 1 and e0 == 0].dma_start(view[r:P:32], ws_rows[e0:e1].rearrange("e (q r) l -> r q e l", r=4)[r])

        def listed(j0, j1):
            return offsets[:, j0 // 16 : j1 // 16]


        nc.vector.tensor_copy(gs[:], xs[:].indirect(listed(0, EARLY_BYTES)))
        nc.vector.tensor_copy(gw_first[:], xw[:].bitcast(U32).indirect(listed(0, CAP)))
        for j0, j1 in ((CAP, BANK), (BANK, SLOTS)):
            nc.vector.tensor_copy(gw[:, j0 - CAP : j1 - CAP], xw[:].bitcast(U32).indirect(listed(j0, j1)))
        gs_late = keep.tile([P, SLOTS - EARLY_BYTES], U8, name="gw_first", align_bytes=64)
        nc.vector.tensor_copy(gs_late[:], xs[:].indirect(listed(EARLY_BYTES, SLOTS)))

        def product(s):
            e = s * P // CAP
            slots = slice(s * P, (s + 1) * P)
            v = ps_y.tile([P, WIDTH], F32, name="v")
            nc.tensor.matmul_mx(
                out=v[:],
                lhsT=(gw_first[:, slots] if e == 0 else gw[:, s * P - CAP : (s + 1) * P - CAP]).bitcast(FP8X4),
                lhsT_scale=gs[:, slots] if s * P < EARLY_BYTES else gs_late[:, s * P - EARLY_BYTES : (s + 1) * P - EARLY_BYTES],
                rhs=(ww_first[:, e, :] if e < FIRST_EXPERTS else ww_rest[:, e - FIRST_EXPERTS, :]).bitcast(FP4X4),
                rhs_scale=ws_first[:, e * WIDTH : (e + 1) * WIDTH] if e < FIRST_EXPERTS else ws_rest[:, (e - FIRST_EXPERTS) * WIDTH : (e - FIRST_EXPERTS + 1) * WIDTH],
                start=True,
                stop=True,
            )
            r = keep.tile([P, PACK, P], F32, name=f"r{s}", align_bytes=64)
            nc.scalar.activation(r[:], v[:].rearrange("j (p d) -> j d p", d=PACK), ACT.Relu)
            return r

        pieces = PIECES
        relu = {}
        ends = [a + CAP for u, j0, j1 in pieces for a in range(j0, j1, P) if a % CAP == 0] + [0]
        step = 0
        for k, (u, j0, j1) in enumerate(pieces):
            stage = keep.tile([P, (j1 - j0) * PAIRS], BF16, name=f"stage{k}", align_bytes=64)
            starts = [a for a in range(j0, j1, P) if k < FINE or a % CAP == 0 or a == j0]
            for a, b in zip(starts, starts[1:] + [j1]):
                unit = b - a
                if a % CAP == 0:
                    step = step + 1
                    for s in range(len(relu), min(TILES, max(LEAD, len(relu) + 1, ends[step] // P))):
                        relu[s] = product(s)
                banks.append(banks.pop(0))
                for s in range(a // P, (a + unit) // P):
                    for e in range(PAIRS):
                        col = e * unit + s * P - a
                        nc.tensor.transpose(banks[0][:, col : col + P], relu[s][:, PAIRS * u + e, :], ident[:])
                y = keep.tile([P, PAIRS, unit], F32, name=f"y{a // P}_{u}", align_bytes=64)
                nc.scalar.activation(y[:].rearrange("p e j -> p (e j)"), banks[0][:, 0 : PAIRS * unit], ACT.Square)
                nc.gpsimd.tensor_tensor(
                    stage[:, (a - j0) * PAIRS : (a - j0 + unit) * PAIRS].rearrange("p (j e) -> p e j", e=PAIRS),
                    y[:],
                    (gates_first[:, a : a + unit] if a < BANK else gates_rest[:, a - BANK : a - BANK + unit]).unsqueeze(1).to_broadcast([P, PAIRS, unit]),
                    MULT,
                )
            nc.vector.tensor_copy(windows[u][:].indirect(listed(j0, j1)), stage[:].bitcast(F32))

        units = [(g, o) for g in range(TOKENS // SPAN) for o in range(HEADS)]
        room = keep.tile([P, len(units) * UNIT_WORDS], U32, name=f"r{TILES - 1}", align_bytes=64)
        aparts = {i: keep.tile([P, PAIRS, SPAN], U32, name=f"r{TILES - 2 - n}", align_bytes=64) for n, i in enumerate(STAGED)}

        def woven(i, dtype):
            return room[:, i * UNIT_WORDS : (i + 1) * UNIT_WORDS].bitcast(dtype)

        def source(u, i, dtype):
            g, o = units[i]
            return windows[u][:, o * TOKENS + g * SPAN : o * TOKENS + (g + 1) * SPAN].bitcast(dtype)

        def target(u, i, dtype):
            if i in STAGED:
                return aparts[i][:].bitcast(dtype)[:, u, :]
            return woven(i, dtype).rearrange("p (t u) -> p t u", u=PAIRS)[:, :, u]

        for i in range(len(units)):
            nc.scalar.copy(target(0, i, U32), source(0, i, U32))

        mw = keep.tile([P, HEADS, N_OUT], I32, name=MW_SLOT, align_bytes=64)
        ms = keep.tile([P, N_OUT], U8, name=MS_SLOT, align_bytes=64)
        nc.gpsimd.memset(ms[:].bitcast(I32), 0)
        ms_rows = wm_scales.bitcast(I32)
        for q in range(4):
            nc.sync.dma_start(ms[32 * q : 32 * q + 16, :].bitcast(I32), ms_rows[:, 4 * q : 4 * q + 4, :])
        mw_rows = wm_words.rearrange("s p n d -> p s (n d)").bitcast(I32)
        for o in reversed(range(HEADS)):
            nc.sync.dma_start(mw[:, o], mw_rows[:, o])

        for i in range(WARM):
            nc.tensor.matmul_mx(
                out=banks[0][:],
                lhsT=mw[:, 0, 0:P].bitcast(FP8X4),
                lhsT_scale=ms[:, 0:P],
                rhs=mw[:, 0, :].bitcast(FP8X4),
                rhs_scale=ms[:],
                start=True,
                stop=True,
            )

        for i in BY_DMA:
            nc.sync.dma_start(target(1, i, I32), source(1, i, I32))

        codes = []
        for i in range(len(units)):
            if i in DIRECT:
                nc.vector.tensor_copy(target(1, i, I32), source(1, i, I32))
            elif i not in BY_DMA:
                nc.scalar.copy(target(1, i, U32), source(1, i, U32))
            if i in STAGED:
                nc.vector.tensor_copy(woven(i, I32).rearrange("p (t u) -> p t u", u=PAIRS), aparts[i][:].bitcast(I32).rearrange("p u t -> p t u"))
            cw = keep.tile([P, SPAN], U32, name=f"cw{i}", align_bytes=64)
            cs = keep.tile([P, SPAN], U8, name=f"cs{i}", align_bytes=64)
            nc.vector.quantize_mx(out=cw[:].bitcast(FP8X4), scales=cs[:], in_=woven(i, BF16))
            codes.append((cw, cs))

        free = [ps_y.tile([P, BANK], F32, name="v") for b in range(5)] + banks
        for g in range(TOKENS // SPAN):
            accs = free[g * ROWS : (g + 1) * ROWS]
            order = [(o, m) for o in range(HEADS - 2) for m in range(ROWS)]
            order.extend((o, m) for m in range(ROWS) for o in range(HEADS - 2, HEADS))
            for o, m in order:
                cols = slice(m * P, (m + 1) * P)
                cw, cs = codes[g * HEADS + o]
                nc.tensor.matmul_mx(
                    out=accs[m][:, 0:SPAN],
                    lhsT=mw[:, o, cols].bitcast(FP8X4),
                    lhsT_scale=ms[4 * o :, cols],
                    rhs=cw[:].bitcast(FP8X4),
                    rhs_scale=cs[:],
                    start=(o == 0),
                    stop=(o == HEADS - 1),
                )
            for m0, m1 in STORES[g]:
                res = ring.tile([P, m1 - m0, SPAN], F32, name="res")
                for m in range(m0, m1):
                    if (g, m) in VECTOR_OUT:
                        nc.vector.tensor_copy(res[:, m - m0], accs[m][:, 0:SPAN])
                    else:
                        nc.scalar.copy(res[:, m - m0], accs[m][:, 0:SPAN])
                nc.sync.dma_start(out.rearrange("(m p) t -> p m t", p=P)[:, m0:m1, g * SPAN : (g + 1) * SPAN], res[:])
